import numpy as np
import ml_dtypes


def mxq(x, axis, fmt="e4m3"):
    dtype, down = {"e4m3": (ml_dtypes.float8_e4m3fn, 7), "e5m2": (ml_dtypes.float8_e5m2, 14)}[fmt]
    v = np.moveaxis(np.asarray(x, np.float32).astype(ml_dtypes.bfloat16).astype(np.float64), axis, -1)
    blocks = v.reshape(v.shape[:-1] + (-1, 32))
    amax = np.abs(blocks).max(-1, keepdims=True)
    byte = np.maximum(np.where(amax > 0, np.frexp(amax)[1] - 1 + 127, 0) - down, 1)
    scale = np.exp2(byte - 127.0)
    codes = (blocks / scale).astype(np.float32).astype(dtype).astype(np.float64)
    return np.moveaxis((codes * scale).reshape(v.shape), -1, axis)


WIDE = False


def mx_kscale(k):
    if not WIDE:
        return np.ones(k)
    levels = np.array([10, -10, 5, -5, 0])
    if k % 512:
        return np.exp2(np.random.permutation(np.resize(levels, k // 32))).repeat(32)
    a = np.empty((k // 512, 16))
    for p in range(k // 512):
        a[p, :8] = np.random.permutation(np.resize(levels, 8))
        for g in range(8):
            far = levels[np.abs(levels - a[p, g]) >= 10]
            a[p, g + 8] = far[np.random.randint(len(far))]
    return np.exp2(a.ravel()).repeat(32)


def f64(x):
    return np.asarray(x).astype(np.float64)


E2M1 = np.array([0.0, 0.5, 1.0, 1.5, 2.0, 3.0, 4.0, 6.0, -0.0, -0.5, -1.0, -1.5, -2.0, -3.0, -4.0, -6.0])


def pack_weight(w, fmt):
    k, n = w.shape
    w = f64(np.asarray(w, np.float32).astype(ml_dtypes.bfloat16)).reshape(k // 32, 32, n)
    amax = np.abs(w).max(1)
    if fmt == "e4m3":
        byte = np.frexp(amax)[1] - 1 + 127 - 7
    else:
        mant, ex = np.frexp(amax / 6.0)
        byte = np.where(mant > 0.5, ex, ex - 1) + 127
    byte = np.clip(np.where(amax > 0, byte, 1), 1, 254)
    scaled = (w * np.exp2(127.0 - byte)[:, None, :]).reshape(k, n).astype(np.float32)
    by_word = np.ascontiguousarray(scaled.reshape(k // 512, 128, 4, n).transpose(0, 1, 3, 2))
    if fmt == "e4m3":
        words = by_word.astype(ml_dtypes.float8_e4m3fn).view(np.uint8)
    else:
        c = by_word.astype(ml_dtypes.float4_e2m1fn).view(np.uint8) & 0xF
        words = (c[..., 0::2] | (c[..., 1::2] << 4)).reshape(k // 512, 128, 2 * n)
    return np.ascontiguousarray(words), np.ascontiguousarray(byte.astype(np.uint8).reshape(k // 512, 16, n))


def unpack_weight(words, scales, fmt):
    g, _, n = scales.shape
    words = np.ascontiguousarray(words).reshape(g, 128, n, -1)
    if fmt == "e4m3":
        vals = words.view(ml_dtypes.float8_e4m3fn).astype(np.float64)
    else:
        nib = np.empty((g, 128, n, 4), np.uint8)
        nib[..., 0::2] = words & 0xF
        nib[..., 1::2] = words >> 4
        vals = E2M1[nib]
    vals = vals * np.repeat(np.exp2(scales.astype(np.float64) - 127.0), 8, axis=1)[..., None]
    return vals.transpose(0, 1, 3, 2).reshape(g * 512, n)


def planes(y):
    n, m = y.shape
    v = y.astype(np.float32).astype(ml_dtypes.bfloat16).astype(np.float64).reshape(n // 32, 32, m)
    top = np.abs(v).max(1)
    byte = np.clip(np.where(top > 0, np.frexp(top)[1] - 1 + 127 - 7, 1), 1, 254)
    codes = (v * np.exp2(127.0 - byte)[:, None, :]).reshape(n, m).astype(np.float32).astype(ml_dtypes.float8_e4m3fn).view(np.uint8)
    words = codes.reshape(n // 512, 128, 4, m).transpose(0, 1, 3, 2)
    return np.ascontiguousarray(words), np.ascontiguousarray(byte.astype(np.uint8).reshape(n // 512, 16, m))


O, K, M, T = 1024, 2560, 1536, 512


def setup_inputs():
    n = np.random.standard_normal
    s = mx_kscale(K)[:, None]
    x = n((K, T)); x[:O] *= 6.0
    w = n((K, M)) / np.sqrt(K) / s; w[:O] /= 2.0
    p_x4 = pack_weight(x[O:] * s[O:], "e2m1")
    p_w4 = pack_weight(w[O:], "e2m1")
    return {
        "x8": (x[:O] * s[:O]).astype(np.float32),
        "w8": (w[:O]).astype(np.float32),
        "x4_words": p_x4[0],
        "x4_scales": p_x4[1],
        "w4_words": p_w4[0],
        "w4_scales": p_w4[1],
    }


def reference(x8, w8, x4_words, x4_scales, w4_words, w4_scales):
    x8_ = mxq(f64(x8), 0, "e4m3")
    w8_ = mxq(f64(w8), 0, "e4m3")
    x4_ = unpack_weight(x4_words, x4_scales, "e2m1")
    w4_ = unpack_weight(w4_words, w4_scales, "e2m1")
    y = x8_.T @ w8_ + x4_.T @ w4_
    out_0 = np.maximum(y, 0.0) ** 2
    return (out_0,) + planes(out_0)

@@ -1,0 +1,267 @@
+from contextlib import ExitStack
+
+import concourse.mybir as mybir
+
+O, K4, N, T = 1024, 1536, 1536, 512
+FLOPS = 2 * (O + K4) * N * T
+
+F32 = mybir.dt.float32
+BF16 = mybir.dt.bfloat16
+I32 = mybir.dt.int32
+U32 = mybir.dt.uint32
+U8 = mybir.dt.uint8
+FP8X4 = mybir.dt.float8_e4m3fn_x4
+FP4X4 = mybir.dt.float4_e2m1fn_x4
+ACT = mybir.ActivationFunctionType
+ALU = mybir.AluOpType
+
+P = 128
+PACK = 4
+K_PASS = P * PACK
+PASSES8 = O // K_PASS
+PASSES4 = K4 // K_PASS
+CH = 512
+CHUNKS = N // CH
+EARLY = 2 * CH
+V_COLS = 384
+
+
+def tile_mix_atom_tm_pl_relu2_kernel(
+    tc, x8, w8, x4_words, x4_scales, w4_words, w4_scales, out_0, out_1, out_2
+):
+    nc = tc.nc
+    with ExitStack() as ctx:
+        sb = ctx.enter_context(tc.tile_pool(name="sb", bufs=1))
+        psum = ctx.enter_context(tc.psum_pool(name="psum", bufs=1))
+        ctx.enter_context(tc.manual_schedule())
+
+        def tile(name, shape, dtype):
+            return sb.tile(shape, dtype, name=name, align_bytes=64)
+
+        x4_raw = tile("x4_raw", [P, PASSES4, 2 * T], U8)
+        x4_codes = tile("x4_codes", [P, PASSES4, PACK, 2 * P], U8)
+        x4s_raw = tile("x4s_raw", [P, PASSES4, T], U8)
+        x4s = tile("x4s", [P, PASSES4, PACK, P], U8)
+        w4_early = tile("w4_early", [P, PASSES4, 2 * EARLY], U8)
+        w4_late = tile("w4_late", [P, PASSES4, 2 * CH], U8)
+        w4s = tile("w4s", [P, PASSES4, N], U8)
+        x8_raw = [tile("x8_raw%d" % g, [P, PACK, T], F32) for g in range(PASSES8)]
+        x8_bf = [tile("x8_bf%d" % g, [P, T * PACK], BF16) for g in range(PASSES8)]
+        x8_codes = [tile("x8_codes%d" % g, [P, T], U32) for g in range(PASSES8)]
+        x8s = [tile("x8s%d" % g, [P, T], U8) for g in range(PASSES8)]
+        keys = [(c, g) for c in range(CHUNKS) for g in range(PASSES8)]
+        w8_raw = {k: tile("w8_raw%d_%d" % k, [P, PACK, CH], F32) for k in keys}
+        w8_bf = {k: tile("w8_bf%d_%d" % k, [P, CH, PACK], BF16) for k in keys}
+        w8_codes = {k: tile("w8_codes%d_%d" % k, [P, CH], U32) for k in keys}
+        w8s = {k: tile("w8s%d_%d" % k, [P, CH], U8) for k in keys}
+        relu = [tile("relu%d" % c, [P, PACK, CH], F32) for c in range(CHUNKS)]
+        res = [tile("res%d" % c, [P, PACK, CH], F32) for c in range(CHUNKS)]
+        res_bf = [tile("res_bf%d" % c, [P, CH, PACK], BF16) for c in range(CHUNKS)]
+        res_codes = tile("res_codes", [P, N], U32)
+        res_scales = tile("res_scales", [P, N], U8)
+        acc = {}
+
+        def load_scales(plane, src, r):
+            rows = src.rearrange("a (q r) n -> r q a n", r=PACK)[r]
+            nc.sync.dma_start(out=plane[r:P:32, :, :].bitcast(I32), in_=rows.bitcast(I32))
+
+        def load_rows(raw, src, g, c0, width):
+            rows = src[g * K_PASS : (g + 1) * K_PASS, c0 : c0 + width]
+            nc.sync.dma_start(out=raw[:], in_=rows.rearrange("(p j) n -> p j n", j=PACK))
+
+        def load_words(dst, src, b0, width):
+            words = src[:, :, b0 : b0 + width].rearrange("a p w -> p a w")
+            nc.sync.dma_start(out=dst[:].bitcast(I32), in_=words.bitcast(I32))
+
+        def group_w8(c, g, engine, c0, c1):
+            dst = w8_bf[c, g][:, c0:c1, :]
+            src = w8_raw[c, g][:, :, c0:c1].rearrange("p j n -> p n j")
+            if engine is nc.vector:
+                nc.vector.tensor_copy(out=dst, in_=src)
+            else:
+                nc.scalar.copy(out=dst, in_=src)
+
+        def quantise_w8(c, g):
+            nc.vector.quantize_mx(
+                out=w8_codes[c, g][:].bitcast(FP8X4),
+                scales=w8s[c, g][:],
+                in_=w8_bf[c, g][:].rearrange("p n j -> p (n j)"),
+            )
+
+        def passes4(c, passes):
+            for a in passes:
+                for r in range(PACK):
+                    if a == 0:
+                        acc[c, r] = psum.tile([P, CH], F32, name="acc%d" % ((c * PACK + r) % 8))
+                    if c < CHUNKS - 1:
+                        moving = w4_early[:, a, 2 * c * CH : 2 * (c + 1) * CH]
+                    else:
+                        moving = w4_late[:, a, :]
+                    nc.tensor.matmul_mx(
+                        out=acc[c, r][:],
+                        lhsT=x4_codes[:, a, r, :].bitcast(FP4X4),
+                        lhsT_scale=x4s[:, a, r, :],
+                        rhs=moving.bitcast(FP4X4),
+                        rhs_scale=w4s[:, a, c * CH : (c + 1) * CH],
+                        start=(a == 0),
+                        stop=False,
+                    )
+
+        def pass8(c, g):
+            for r in range(PACK):
+                nc.tensor.matmul_mx(
+                    out=acc[c, r][:],
+                    lhsT=x8_codes[g][:, r * P : (r + 1) * P].bitcast(FP8X4),
+                    lhsT_scale=x8s[g][:, r * P : (r + 1) * P],
+                    rhs=w8_codes[c, g][:].bitcast(FP8X4),
+                    rhs_scale=w8s[c, g][:],
+                    start=False,
+                    stop=(g == PASSES8 - 1),
+                )
+
+        def rectify(c, r, engine):
+            if engine is nc.vector:
+                nc.vector.tensor_scalar(
+                    out=relu[c][:, r, :], in0=acc[c, r][:], scalar1=0.0, scalar2=None, op0=ALU.max
+                )
+            else:
+                nc.scalar.activation(out=relu[c][:, r, :], in_=acc[c, r][:], func=ACT.Relu)
+
+        def square(c, r, engine):
+            if engine is nc.vector:
+                nc.vector.tensor_tensor(
+                    out=res[c][:, r, :], in0=relu[c][:, r, :], in1=relu[c][:, r, :], op=ALU.mult
+                )
+            else:
+                nc.scalar.activation(out=res[c][:, r, :], in_=relu[c][:, r, :], func=ACT.Square)
+
+        def group_res(c, engine, c0, c1):
+            dst = res_bf[c][:, c0:c1, :]
+            src = res[c][:, :, c0:c1].rearrange("p r n -> p n r")
+            if engine is nc.vector:
+                nc.vector.tensor_copy(out=dst, in_=src)
+            else:
+                nc.scalar.copy(out=dst, in_=src)
+
+        def quantise_res(c):
+            nc.vector.quantize_mx(
+                out=res_codes[:, c * CH : (c + 1) * CH].bitcast(FP8X4),
+                scales=res_scales[:, c * CH : (c + 1) * CH],
+                in_=res_bf[c][:].rearrange("p n r -> p (n r)"),
+            )
+
+        out_rows = out_0.rearrange("(p r) n -> p r n", r=PACK)
+        out_words = out_1[0].rearrange("p n i -> p (n i)").bitcast(I32)
+
+        nc.vector.memset(x4s_raw[:].bitcast(I32), 0)
+        nc.vector.memset(w4s[:].bitcast(I32), 0)
+
+        load_words(x4_raw, x4_words, 0, 2 * T)
+        load_rows(x8_raw[0], x8, 0, 0, T)
+        for r in range(PACK):
+            load_scales(x4s_raw, x4_scales, r)
+        load_scales(w4s, w4_scales, 0)
+        load_rows(x8_raw[1], x8, 1, 0, T)
+        for r in range(1, PACK):
+            load_scales(w4s, w4_scales, r)
+        load_words(w4_early, w4_words, 0, 2 * EARLY)
+        for c in range(CHUNKS):
+            if c == CHUNKS - 1:
+                load_words(w4_late, w4_words, 2 * EARLY, 2 * CH)
+            for g in range(PASSES8):
+                load_rows(w8_raw[c, g], w8, g, c * CH, CH)
+
+        for a in range(PASSES4):
+            nc.vector.tensor_copy(
+                out=x4_codes[:, a, :, :].rearrange("p r (m b) -> p r m b", b=2),
+                in_=x4_raw[:, a, :].rearrange("p (m r b) -> p r m b", r=PACK, b=2),
+            )
+        nc.scalar.activation(
+            out=x8_bf[0][:].rearrange("p (r m j) -> p r m j", r=PACK, j=PACK),
+            in_=x8_raw[0][:].rearrange("p j (m r) -> p r m j", r=PACK),
+            func=ACT.Copy,
+        )
+        nc.vector.tensor_copy(
+            out=x4s[:], in_=x4s_raw[:].rearrange("p a (m r) -> p a r m", r=PACK)
+        )
+        nc.vector.tensor_copy(
+            out=x8_bf[1][:].rearrange("p (r m j) -> p r m j", r=PACK, j=PACK),
+            in_=x8_raw[1][:].rearrange("p j (m r) -> p r m j", r=PACK),
+        )
+        for g in range(PASSES8):
+            nc.vector.quantize_mx(
+                out=x8_codes[g][:].bitcast(FP8X4), scales=x8s[g][:], in_=x8_bf[g][:]
+            )
+
+        V, S = nc.vector, nc.scalar
+
+        def prep(c, g, v_cols):
+            if v_cols < CH:
+                group_w8(c, g, S, v_cols, CH)
+            group_w8(c, g, V, 0, v_cols)
+
+        def store_rows(c, r0, r1):
+            nc.sync.dma_start(out=out_rows[:, r0:r1, c * CH : (c + 1) * CH], in_=res[c][:, r0:r1, :])
+
+        def store_words(c):
+            cols = slice(c * CH, (c + 1) * CH)
+            nc.sync.dma_start(out=out_words[:, cols], in_=res_codes[:, cols].bitcast(I32))
+
+        passes4(0, range(PASSES4))
+        prep(0, 0, 352)
+        quantise_w8(0, 0)
+        pass8(0, 0)
+        passes4(1, [0])
+        prep(0, 1, 352)
+        quantise_w8(0, 1)
+        pass8(0, 1)
+        passes4(1, [1, 2])
+
+        for r in range(PACK):
+            rectify(0, r, S)
+        square(0, 0, S)
+        prep(1, 0, CH)
+        quantise_w8(1, 0)
+        pass8(1, 0)
+        prep(1, 1, 384)
+        quantise_w8(1, 1)
+        pass8(1, 1)
+        for r in range(1, PACK):
+            square(0, r, S)
+        store_rows(0, 0, PACK)
+        passes4(2, range(PASSES4))
+        for r in range(PACK):
+            rectify(1, r, S)
+        group_res(0, V, 0, CH)
+        prep(2, 0, CH)
+        quantise_res(0)
+        store_words(0)
+        quantise_w8(2, 0)
+        pass8(2, 0)
+        for r in range(PACK - 1):
+            square(1, r, S)
+        prep(2, 1, 384)
+        quantise_w8(2, 1)
+        pass8(2, 1)
+        square(1, PACK - 1, S)
+        store_rows(1, 0, PACK)
+        group_res(1, S, 256, CH)
+        group_res(1, V, 0, 256)
+        rectify(2, 0, S)
+        rectify(2, 1, S)
+        quantise_res(1)
+        store_words(1)
+        rectify(2, 2, S)
+        rectify(2, 3, S)
+        for r in range(PACK):
+            square(2, r, [V,V,V,S][r])
+            store_rows(2, r, r + 1)
+        group_res(2, S, 352, CH)
+        group_res(2, V, 0, 352)
+        quantise_res(2)
+        store_words(2)
+        scale_rows = out_2[0].rearrange("(q r) n -> r q n", r=PACK)
+        for r in range(PACK):
+            nc.scalar.dma_start(
+                out=scale_rows[r].bitcast(I32), in_=res_scales[r:P:32, :].bitcast(I32)
+            )

@@ -63,7 +63,7 @@ def tile_mix_atom_tm_pl_relu2_kernel(
 
         def load_scales(plane, src, r):
             rows = src.rearrange("a (q r) n -> r q a n", r=PACK)[r]
-            nc.sync.dma_start(out=plane[r:P:32, :, :].bitcast(I32), in_=rows.bitcast(I32))
+            nc.gpsimd.dma_start(out=plane[r:P:32, :, :].bitcast(I32), in_=rows.bitcast(I32))
 
         def load_rows(raw, src, g, c0, width):
             rows = src[g * K_PASS : (g + 1) * K_PASS, c0 : c0 + width]
@@ -74,8 +74,8 @@ def tile_mix_atom_tm_pl_relu2_kernel(
             nc.sync.dma_start(out=dst[:].bitcast(I32), in_=words.bitcast(I32))
 
         def group_w8(c, g, engine, c0, c1):
-            dst = w8_bf[c, g][:, c0:c1, :]
-            src = w8_raw[c, g][:, :, c0:c1].rearrange("p j n -> p n j")
+            dst = w8_bf[c, g][:, c0:c1, :].rearrange("p (m i) j -> p m j i", i=PACK)
+            src = w8_raw[c, g][:, :, c0:c1].rearrange("p j (m i) -> p m j i", i=PACK)
             if engine is nc.vector:
                 nc.vector.tensor_copy(out=dst, in_=src)
             else:
@@ -136,8 +136,8 @@ def tile_mix_atom_tm_pl_relu2_kernel(
                 nc.scalar.activation(out=res[c][:, r, :], in_=relu[c][:, r, :], func=ACT.Square)
 
         def group_res(c, engine, c0, c1):
-            dst = res_bf[c][:, c0:c1, :]
-            src = res[c][:, :, c0:c1].rearrange("p r n -> p n r")
+            dst = res_bf[c][:, c0:c1, :].rearrange("p (m i) r -> p m r i", i=PACK)
+            src = res[c][:, :, c0:c1].rearrange("p r (m i) -> p m r i", i=PACK)
             if engine is nc.vector:
                 nc.vector.tensor_copy(out=dst, in_=src)
             else:
@@ -156,14 +156,13 @@ def tile_mix_atom_tm_pl_relu2_kernel(
         nc.vector.memset(x4s_raw[:].bitcast(I32), 0)
         nc.vector.memset(w4s[:].bitcast(I32), 0)
 
-        load_words(x4_raw, x4_words, 0, 2 * T)
-        load_rows(x8_raw[0], x8, 0, 0, T)
         for r in range(PACK):
             load_scales(x4s_raw, x4_scales, r)
-        load_scales(w4s, w4_scales, 0)
-        load_rows(x8_raw[1], x8, 1, 0, T)
-        for r in range(1, PACK):
+        for r in range(PACK):
             load_scales(w4s, w4_scales, r)
+        for g in range(PASSES8):
+            load_rows(x8_raw[g], x8, g, 0, T)
+        load_words(x4_raw, x4_words, 0, 2 * T)
         load_words(w4_early, w4_words, 0, 2 * EARLY)
         for c in range(CHUNKS):
             if c == CHUNKS - 1:
@@ -171,29 +170,27 @@ def tile_mix_atom_tm_pl_relu2_kernel(
             for g in range(PASSES8):
                 load_rows(w8_raw[c, g], w8, g, c * CH, CH)
 
+        for g in range(PASSES8):
+            nc.scalar.activation(
+                out=x8_bf[g][:].rearrange("p (r m j) -> p r m j", r=PACK, j=PACK),
+                in_=x8_raw[g][:].rearrange("p j (m r) -> p r m j", r=PACK),
+                func=ACT.Copy,
+            )
+        nc.vector.tensor_copy(
+            out=x4s[:], in_=x4s_raw[:].rearrange("p a (m r) -> p a r m", r=PACK)
+        )
         for a in range(PASSES4):
             nc.vector.tensor_copy(
                 out=x4_codes[:, a, :, :].rearrange("p r (m b) -> p r m b", b=2),
                 in_=x4_raw[:, a, :].rearrange("p (m r b) -> p r m b", r=PACK, b=2),
             )
-        nc.scalar.activation(
-            out=x8_bf[0][:].rearrange("p (r m j) -> p r m j", r=PACK, j=PACK),
-            in_=x8_raw[0][:].rearrange("p j (m r) -> p r m j", r=PACK),
-            func=ACT.Copy,
-        )
-        nc.vector.tensor_copy(
-            out=x4s[:], in_=x4s_raw[:].rearrange("p a (m r) -> p a r m", r=PACK)
-        )
-        nc.vector.tensor_copy(
-            out=x8_bf[1][:].rearrange("p (r m j) -> p r m j", r=PACK, j=PACK),
-            in_=x8_raw[1][:].rearrange("p j (m r) -> p r m j", r=PACK),
-        )
         for g in range(PASSES8):
             nc.vector.quantize_mx(
                 out=x8_codes[g][:].bitcast(FP8X4), scales=x8s[g][:], in_=x8_bf[g][:]
             )
 
         V, S = nc.vector, nc.scalar
+        scale_rows = out_2[0].rearrange("(q r) n -> r q n", r=PACK)
 
         def prep(c, g, v_cols):
             if v_cols < CH:
@@ -203,9 +200,24 @@ def tile_mix_atom_tm_pl_relu2_kernel(
         def store_rows(c, r0, r1):
             nc.sync.dma_start(out=out_rows[:, r0:r1, c * CH : (c + 1) * CH], in_=res[c][:, r0:r1, :])
 
-        def store_words(c):
-            cols = slice(c * CH, (c + 1) * CH)
+        def store_words(c0, c1):
+            cols = slice(c0 * CH, c1 * CH)
             nc.sync.dma_start(out=out_words[:, cols], in_=res_codes[:, cols].bitcast(I32))
+
+        def store_scales(c0, c1, queue):
+            cols = slice(c0 * CH, c1 * CH)
+            for r in range(PACK):
+                queue.dma_start(
+                    out=scale_rows[r][:, cols].bitcast(I32),
+                    in_=res_scales[r:P:32, cols].bitcast(I32),
+                )
+
+        def finish(c):
+            rectify(c, 0, S)
+            for r in range(PACK):
+                if r + 1 < PACK:
+                    rectify(c, r + 1, S)
+                square(c, r, S)
 
         passes4(0, range(PASSES4))
         prep(0, 0, 352)
@@ -216,52 +228,47 @@ def tile_mix_atom_tm_pl_relu2_kernel(
         quantise_w8(0, 1)
         pass8(0, 1)
         passes4(1, [1, 2])
+        finish(0)
+        store_rows(0, 0, PACK)
 
-        for r in range(PACK):
-            rectify(0, r, S)
-        square(0, 0, S)
         prep(1, 0, CH)
         quantise_w8(1, 0)
         pass8(1, 0)
-        prep(1, 1, 384)
+        prep(1, 1, CH)
         quantise_w8(1, 1)
         pass8(1, 1)
-        for r in range(1, PACK):
-            square(0, r, S)
-        store_rows(0, 0, PACK)
         passes4(2, range(PASSES4))
-        for r in range(PACK):
-            rectify(1, r, S)
+        finish(1)
+        store_rows(1, 0, 2)
+        store_rows(1, 2, PACK)
+
         group_res(0, V, 0, CH)
         prep(2, 0, CH)
         quantise_res(0)
-        store_words(0)
         quantise_w8(2, 0)
         pass8(2, 0)
-        for r in range(PACK - 1):
-            square(1, r, S)
-        prep(2, 1, 384)
+        prep(2, 1, CH)
         quantise_w8(2, 1)
         pass8(2, 1)
-        square(1, PACK - 1, S)
-        store_rows(1, 0, PACK)
+
         group_res(1, S, 256, CH)
         group_res(1, V, 0, 256)
         rectify(2, 0, S)
-        rectify(2, 1, S)
         quantise_res(1)
-        store_words(1)
+        store_words(0, 2)
+        rectify(2, 1, S)
+        square(2, 0, V)
+        store_rows(2, 0, 1)
         rectify(2, 2, S)
-        rectify(2, 3, S)
-        for r in range(PACK):
-            square(2, r, [V,V,V,S][r])
-            store_rows(2, r, r + 1)
+        rectify(2, 3, V)
+        square(2, 1, S)
+        store_rows(2, 1, 2)
+        square(2, 2, V)
+        store_rows(2, 2, 3)
+        square(2, 3, S)
+        store_rows(2, 3, 4)
         group_res(2, S, 352, CH)
         group_res(2, V, 0, 352)
         quantise_res(2)
-        store_words(2)
-        scale_rows = out_2[0].rearrange("(q r) n -> r q n", r=PACK)
-        for r in range(PACK):
-            nc.scalar.dma_start(
-                out=scale_rows[r].bitcast(I32), in_=res_scales[r:P:32, :].bitcast(I32)
-            )
+        store_words(2, 3)
+        store_scales(0, 3, nc.scalar)

@@ -61,9 +61,9 @@ def tile_mix_atom_tm_pl_relu2_kernel(
         res_scales = tile("res_scales", [P, N], U8)
         acc = {}
 
-        def load_scales(plane, src, r):
+        def load_scales(plane, src, r, queue):
             rows = src.rearrange("a (q r) n -> r q a n", r=PACK)[r]
-            nc.gpsimd.dma_start(out=plane[r:P:32, :, :].bitcast(I32), in_=rows.bitcast(I32))
+            queue.dma_start(out=plane[r:P:32, :, :].bitcast(I32), in_=rows.bitcast(I32))
 
         def load_rows(raw, src, g, c0, width):
             rows = src[g * K_PASS : (g + 1) * K_PASS, c0 : c0 + width]
@@ -157,36 +157,39 @@ def tile_mix_atom_tm_pl_relu2_kernel(
         nc.vector.memset(w4s[:].bitcast(I32), 0)
 
         for r in range(PACK):
-            load_scales(x4s_raw, x4_scales, r)
-        for r in range(PACK):
-            load_scales(w4s, w4_scales, r)
-        for g in range(PASSES8):
-            load_rows(x8_raw[g], x8, g, 0, T)
+            load_scales(w4s, w4_scales, r, nc.gpsimd)
         load_words(x4_raw, x4_words, 0, 2 * T)
+        for r in range(PACK):
+            load_scales(x4s_raw, x4_scales, r, nc.sync)
         load_words(w4_early, w4_words, 0, 2 * EARLY)
         for c in range(CHUNKS):
             if c == CHUNKS - 1:
                 load_words(w4_late, w4_words, 2 * EARLY, 2 * CH)
             for g in range(PASSES8):
+                if c == 0:
+                    load_rows(x8_raw[g], x8, g, 0, T)
                 load_rows(w8_raw[c, g], w8, g, c * CH, CH)
 
-        for g in range(PASSES8):
-            nc.scalar.activation(
-                out=x8_bf[g][:].rearrange("p (r m j) -> p r m j", r=PACK, j=PACK),
-                in_=x8_raw[g][:].rearrange("p j (m r) -> p r m j", r=PACK),
-                func=ACT.Copy,
+        def group_x8(g, engine, m0, m1):
+            dst = x8_bf[g][:].rearrange("p (r m j) -> p m j r", r=PACK, j=PACK)[:, m0:m1, :, :]
+            src = x8_raw[g][:].rearrange("p j (m r) -> p m j r", r=PACK)[:, m0:m1, :, :]
+            if engine is nc.vector:
+                nc.vector.tensor_copy(out=dst, in_=src)
+            else:
+                nc.scalar.activation(out=dst, in_=src, func=ACT.Copy)
+
+        def quantise_x8(g):
+            nc.vector.quantize_mx(
+                out=x8_codes[g][:].bitcast(FP8X4), scales=x8s[g][:], in_=x8_bf[g][:]
             )
-        nc.vector.tensor_copy(
-            out=x4s[:], in_=x4s_raw[:].rearrange("p a (m r) -> p a r m", r=PACK)
-        )
+
         for a in range(PASSES4):
             nc.vector.tensor_copy(
                 out=x4_codes[:, a, :, :].rearrange("p r (m b) -> p r m b", b=2),
                 in_=x4_raw[:, a, :].rearrange("p (m r b) -> p r m b", r=PACK, b=2),
             )
-        for g in range(PASSES8):
-            nc.vector.quantize_mx(
-                out=x8_codes[g][:].bitcast(FP8X4), scales=x8s[g][:], in_=x8_bf[g][:]
+            nc.vector.tensor_copy(
+                out=x4s[:, a, :, :], in_=x4s_raw[:, a, :].rearrange("p (m r) -> p r m", r=PACK)
             )
 
         V, S = nc.vector, nc.scalar
@@ -220,14 +223,19 @@ def tile_mix_atom_tm_pl_relu2_kernel(
                 square(c, r, S)
 
         passes4(0, range(PASSES4))
-        prep(0, 0, 352)
+        passes4(1, [0, 1])
+        group_x8(0, S, 0, P)
+        prep(0, 0, 256)
+        quantise_x8(0)
         quantise_w8(0, 0)
         pass8(0, 0)
-        passes4(1, [0])
+        passes4(1, [2])
+        group_x8(1, S, 64, P)
+        group_x8(1, V, 0, 64)
+        quantise_x8(1)
         prep(0, 1, 352)
         quantise_w8(0, 1)
         pass8(0, 1)
-        passes4(1, [1, 2])
         finish(0)
         store_rows(0, 0, PACK)
 

@@ -61,9 +61,9 @@ def tile_mix_atom_tm_pl_relu2_kernel(
         res_scales = tile("res_scales", [P, N], U8)
         acc = {}
 
-        def load_scales(plane, src, r, queue):
+        def load_scales(plane, src, r):
             rows = src.rearrange("a (q r) n -> r q a n", r=PACK)[r]
-            queue.dma_start(out=plane[r:P:32, :, :].bitcast(I32), in_=rows.bitcast(I32))
+            nc.sync.dma_start(out=plane[r:P:32, :, :].bitcast(I32), in_=rows.bitcast(I32))
 
         def load_rows(raw, src, g, c0, width):
             rows = src[g * K_PASS : (g + 1) * K_PASS, c0 : c0 + width]
@@ -143,11 +143,11 @@ def tile_mix_atom_tm_pl_relu2_kernel(
             else:
                 nc.scalar.copy(out=dst, in_=src)
 
-        def quantise_res(c):
+        def quantise_res(c, c0=0, c1=CH):
             nc.vector.quantize_mx(
-                out=res_codes[:, c * CH : (c + 1) * CH].bitcast(FP8X4),
-                scales=res_scales[:, c * CH : (c + 1) * CH],
-                in_=res_bf[c][:].rearrange("p n r -> p (n r)"),
+                out=res_codes[:, c * CH + c0 : c * CH + c1].bitcast(FP8X4),
+                scales=res_scales[:, c * CH + c0 : c * CH + c1],
+                in_=res_bf[c][:, c0:c1, :].rearrange("p n r -> p (n r)"),
             )
 
         out_rows = out_0.rearrange("(p r) n -> p r n", r=PACK)
@@ -156,11 +156,11 @@ def tile_mix_atom_tm_pl_relu2_kernel(
         nc.vector.memset(x4s_raw[:].bitcast(I32), 0)
         nc.vector.memset(w4s[:].bitcast(I32), 0)
 
-        for r in range(PACK):
-            load_scales(w4s, w4_scales, r, nc.gpsimd)
         load_words(x4_raw, x4_words, 0, 2 * T)
         for r in range(PACK):
-            load_scales(x4s_raw, x4_scales, r, nc.sync)
+            load_scales(x4s_raw, x4_scales, r)
+        for r in range(PACK):
+            load_scales(w4s, w4_scales, r)
         load_words(w4_early, w4_words, 0, 2 * EARLY)
         for c in range(CHUNKS):
             if c == CHUNKS - 1:
@@ -204,7 +204,7 @@ def tile_mix_atom_tm_pl_relu2_kernel(
             nc.sync.dma_start(out=out_rows[:, r0:r1, c * CH : (c + 1) * CH], in_=res[c][:, r0:r1, :])
 
         def store_words(c0, c1):
-            cols = slice(c0 * CH, c1 * CH)
+            cols = slice(c0, c1)
             nc.sync.dma_start(out=out_words[:, cols], in_=res_codes[:, cols].bitcast(I32))
 
         def store_scales(c0, c1, queue):
@@ -225,7 +225,7 @@ def tile_mix_atom_tm_pl_relu2_kernel(
         passes4(0, range(PASSES4))
         passes4(1, [0, 1])
         group_x8(0, S, 0, P)
-        prep(0, 0, 256)
+        prep(0, 0, 320)
         quantise_x8(0)
         quantise_w8(0, 0)
         pass8(0, 0)
@@ -236,34 +236,44 @@ def tile_mix_atom_tm_pl_relu2_kernel(
         prep(0, 1, 352)
         quantise_w8(0, 1)
         pass8(0, 1)
-        finish(0)
-        store_rows(0, 0, PACK)
+        for r in range(PACK):
+            rectify(0, r, S)
+        group_w8(1, 0, V, 0, CH)
 
-        prep(1, 0, CH)
         quantise_w8(1, 0)
         pass8(1, 0)
-        prep(1, 1, CH)
+        square(0, 0, S)
+        prep(1, 1, 512)
         quantise_w8(1, 1)
         pass8(1, 1)
+        square(0, 1, S)
+        square(0, 2, S)
+        square(0, 3, S)
+        store_rows(0, 0, PACK)
         passes4(2, range(PASSES4))
-        finish(1)
-        store_rows(1, 0, 2)
-        store_rows(1, 2, PACK)
-
-        group_res(0, V, 0, CH)
-        prep(2, 0, CH)
+        group_res(0, S, 384, CH)
+        group_res(0, V, 0, 384)
+        for r in range(PACK):
+            rectify(1, r, S)
+        group_w8(2, 0, V, 0, CH)
         quantise_res(0)
         quantise_w8(2, 0)
         pass8(2, 0)
-        prep(2, 1, CH)
+        square(1, 0, S)
+        square(1, 1, S)
+        store_rows(1, 0, 2)
+        square(1, 2, S)
+        square(1, 3, S)
+        prep(2, 1, 512)
         quantise_w8(2, 1)
         pass8(2, 1)
 
+        store_rows(1, 2, PACK)
         group_res(1, S, 256, CH)
         group_res(1, V, 0, 256)
         rectify(2, 0, S)
         quantise_res(1)
-        store_words(0, 2)
+        store_words(0, 2 * CH)
         rectify(2, 1, S)
         square(2, 0, V)
         store_rows(2, 0, 1)
@@ -276,7 +286,10 @@ def tile_mix_atom_tm_pl_relu2_kernel(
         square(2, 3, S)
         store_rows(2, 3, 4)
         group_res(2, S, 352, CH)
-        group_res(2, V, 0, 352)
-        quantise_res(2)
-        store_words(2, 3)
+        group_res(2, V, 0, CH // 2)
+        group_res(2, V, CH // 2, 352)
+        quantise_res(2, 0, CH // 2)
+        store_words(2 * CH, 2 * CH + CH // 2)
+        quantise_res(2, CH // 2, CH)
+        store_words(2 * CH + CH // 2, N)
         store_scales(0, 3, nc.scalar)

@@ -61,9 +61,9 @@ def tile_mix_atom_tm_pl_relu2_kernel(
         res_scales = tile("res_scales", [P, N], U8)
         acc = {}
 
-        def load_scales(plane, src, r):
+        def load_scales(plane, src, r, queue):
             rows = src.rearrange("a (q r) n -> r q a n", r=PACK)[r]
-            nc.sync.dma_start(out=plane[r:P:32, :, :].bitcast(I32), in_=rows.bitcast(I32))
+            queue.dma_start(out=plane[r:P:32, :, :].bitcast(I32), in_=rows.bitcast(I32))
 
         def load_rows(raw, src, g, c0, width):
             rows = src[g * K_PASS : (g + 1) * K_PASS, c0 : c0 + width]
@@ -153,15 +153,16 @@ def tile_mix_atom_tm_pl_relu2_kernel(
         out_rows = out_0.rearrange("(p r) n -> p r n", r=PACK)
         out_words = out_1[0].rearrange("p n i -> p (n i)").bitcast(I32)
 
-        nc.vector.memset(x4s_raw[:].bitcast(I32), 0)
         nc.vector.memset(w4s[:].bitcast(I32), 0)
+        nc.vector.memset(x4s_raw[:].bitcast(I32), 0)
 
-        load_words(x4_raw, x4_words, 0, 2 * T)
-        for r in range(PACK):
-            load_scales(x4s_raw, x4_scales, r)
-        for r in range(PACK):
-            load_scales(w4s, w4_scales, r)
+        for r in range(PACK - 1):
+            load_scales(w4s, w4_scales, r, nc.gpsimd)
         load_words(w4_early, w4_words, 0, 2 * EARLY)
+        load_scales(w4s, w4_scales, PACK - 1, nc.sync)
+        for r in range(PACK):
+            load_scales(x4s_raw, x4_scales, r, nc.sync)
+        load_words(x4_raw, x4_words, 0, 2 * T)
         for c in range(CHUNKS):
             if c == CHUNKS - 1:
                 load_words(w4_late, w4_words, 2 * EARLY, 2 * CH)
@@ -223,19 +224,19 @@ def tile_mix_atom_tm_pl_relu2_kernel(
                 square(c, r, S)
 
         passes4(0, range(PASSES4))
-        passes4(1, [0, 1])
         group_x8(0, S, 0, P)
-        prep(0, 0, 320)
+        prep(0, 0, 256)
         quantise_x8(0)
         quantise_w8(0, 0)
         pass8(0, 0)
-        passes4(1, [2])
+        passes4(1, [0])
         group_x8(1, S, 64, P)
         group_x8(1, V, 0, 64)
         quantise_x8(1)
         prep(0, 1, 352)
         quantise_w8(0, 1)
         pass8(0, 1)
+        passes4(1, [1, 2])
         for r in range(PACK):
             rectify(0, r, S)
         group_w8(1, 0, V, 0, CH)
@@ -269,11 +270,12 @@ def tile_mix_atom_tm_pl_relu2_kernel(
         pass8(2, 1)
 
         store_rows(1, 2, PACK)
+        store_words(0, CH)
         group_res(1, S, 256, CH)
         group_res(1, V, 0, 256)
         rectify(2, 0, S)
         quantise_res(1)
-        store_words(0, 2 * CH)
+        store_words(CH, 2 * CH)
         rectify(2, 1, S)
         square(2, 0, V)
         store_rows(2, 0, 1)

@@ -9,6 +9,7 @@ F32 = mybir.dt.float32
 BF16 = mybir.dt.bfloat16
 I32 = mybir.dt.int32
 U32 = mybir.dt.uint32
+U16 = mybir.dt.uint16
 U8 = mybir.dt.uint8
 FP8X4 = mybir.dt.float8_e4m3fn_x4
 FP4X4 = mybir.dt.float4_e2m1fn_x4
@@ -20,10 +21,11 @@ PACK = 4
 K_PASS = P * PACK
 PASSES8 = O // K_PASS
 PASSES4 = K4 // K_PASS
-CH = 512
-CHUNKS = N // CH
-EARLY = 2 * CH
-V_COLS = 384
+BANK = 512
+PIECES = [(n, n + 256) for n in range(0, N, 256)]
+W4_LOADS = [(n, n + 512) for n in range(0, N, 512)]
+W8_LOADS = [W4_LOADS, PIECES]
+STORES = W4_LOADS
 
 
 def tile_mix_atom_tm_pl_relu2_kernel(
@@ -34,6 +36,7 @@ def tile_mix_atom_tm_pl_relu2_kernel(
         sb = ctx.enter_context(tc.tile_pool(name="sb", bufs=1))
         psum = ctx.enter_context(tc.psum_pool(name="psum", bufs=1))
         ctx.enter_context(tc.manual_schedule())
+        V, S = nc.vector, nc.scalar
 
         def tile(name, shape, dtype):
             return sb.tile(shape, dtype, name=name, align_bytes=64)
@@ -42,256 +45,285 @@ def tile_mix_atom_tm_pl_relu2_kernel(
         x4_codes = tile("x4_codes", [P, PASSES4, PACK, 2 * P], U8)
         x4s_raw = tile("x4s_raw", [P, PASSES4, T], U8)
         x4s = tile("x4s", [P, PASSES4, PACK, P], U8)
-        w4_early = tile("w4_early", [P, PASSES4, 2 * EARLY], U8)
-        w4_late = tile("w4_late", [P, PASSES4, 2 * CH], U8)
+        w4_parts = [
+            tile("w4_part%d" % i, [P, PASSES4, 2 * (n1 - n0)], U8) for i, (n0, n1) in enumerate(W4_LOADS)
+        ]
         w4s = tile("w4s", [P, PASSES4, N], U8)
         x8_raw = [tile("x8_raw%d" % g, [P, PACK, T], F32) for g in range(PASSES8)]
         x8_bf = [tile("x8_bf%d" % g, [P, T * PACK], BF16) for g in range(PASSES8)]
         x8_codes = [tile("x8_codes%d" % g, [P, T], U32) for g in range(PASSES8)]
         x8s = [tile("x8s%d" % g, [P, T], U8) for g in range(PASSES8)]
-        keys = [(c, g) for c in range(CHUNKS) for g in range(PASSES8)]
-        w8_raw = {k: tile("w8_raw%d_%d" % k, [P, PACK, CH], F32) for k in keys}
-        w8_bf = {k: tile("w8_bf%d_%d" % k, [P, CH, PACK], BF16) for k in keys}
-        w8_codes = {k: tile("w8_codes%d_%d" % k, [P, CH], U32) for k in keys}
-        w8s = {k: tile("w8s%d_%d" % k, [P, CH], U8) for k in keys}
-        relu = [tile("relu%d" % c, [P, PACK, CH], F32) for c in range(CHUNKS)]
-        res = [tile("res%d" % c, [P, PACK, CH], F32) for c in range(CHUNKS)]
-        res_bf = [tile("res_bf%d" % c, [P, CH, PACK], BF16) for c in range(CHUNKS)]
+        w8_raw = {
+            (g, n0): tile("w8_raw%d_%d" % (g, n0), [P, PACK, n1 - n0], F32)
+            for g in range(PASSES8)
+            for n0, n1 in W8_LOADS[g]
+        }
+        width = [n1 - n0 for n0, n1 in PIECES]
+        keys = [(h, g) for h in range(len(PIECES)) for g in range(PASSES8)]
+        w8_bf = {k: tile("w8_bf%d_%d" % k, [P, width[k[0]], PACK], BF16) for k in keys}
+        w8_codes = {k: tile("w8_codes%d_%d" % k, [P, width[k[0]]], U32) for k in keys}
+        w8s = {k: tile("w8s%d_%d" % k, [P, width[k[0]]], U8) for k in keys}
+        relu = [tile("relu%d" % h, [P, PACK, w], F32) for h, w in enumerate(width)]
+        res = [tile("res%d" % i, [P, PACK, n1 - n0], F32) for i, (n0, n1) in enumerate(STORES)]
+        res_bf = [tile("res_bf%d" % h, [P, w, PACK], BF16) for h, w in enumerate(width)]
         res_codes = tile("res_codes", [P, N], U32)
         res_scales = tile("res_scales", [P, N], U8)
         acc = {}
+
+        out_rows = out_0.rearrange("(p r) n -> p r n", r=PACK)
+        out_words = out_1[0].rearrange("p n i -> p (n i)").bitcast(I32)
+        scale_rows = out_2[0].rearrange("(q r) n -> r q n", r=PACK)
 
         def load_scales(plane, src, r, queue):
             rows = src.rearrange("a (q r) n -> r q a n", r=PACK)[r]
             queue.dma_start(out=plane[r:P:32, :, :].bitcast(I32), in_=rows.bitcast(I32))
 
-        def load_rows(raw, src, g, c0, width):
-            rows = src[g * K_PASS : (g + 1) * K_PASS, c0 : c0 + width]
+        def load_rows(raw, src, g, n0, n1):
+            rows = src[g * K_PASS : (g + 1) * K_PASS, n0:n1]
             nc.sync.dma_start(out=raw[:], in_=rows.rearrange("(p j) n -> p j n", j=PACK))
 
-        def load_words(dst, src, b0, width):
-            words = src[:, :, b0 : b0 + width].rearrange("a p w -> p a w")
+        def load_x8(g):
+            load_rows(x8_raw[g], x8, g, 0, T)
+
+        def load_w8(g, i):
+            n0, n1 = W8_LOADS[g][i]
+            load_rows(w8_raw[g, n0], w8, g, n0, n1)
+
+        def load_words(dst, src, n0, n1):
+            words = src[:, :, 2 * n0 : 2 * n1].rearrange("a p w -> p a w")
             nc.sync.dma_start(out=dst[:].bitcast(I32), in_=words.bitcast(I32))
 
-        def group_w8(c, g, engine, c0, c1):
-            dst = w8_bf[c, g][:, c0:c1, :].rearrange("p (m i) j -> p m j i", i=PACK)
-            src = w8_raw[c, g][:, :, c0:c1].rearrange("p j (m i) -> p m j i", i=PACK)
-            if engine is nc.vector:
-                nc.vector.tensor_copy(out=dst, in_=src)
-            else:
-                nc.scalar.copy(out=dst, in_=src)
+        def load_w4(i):
+            load_words(w4_parts[i], w4_words, W4_LOADS[i][0], W4_LOADS[i][1])
 
-        def quantise_w8(c, g):
-            nc.vector.quantize_mx(
-                out=w8_codes[c, g][:].bitcast(FP8X4),
-                scales=w8s[c, g][:],
-                in_=w8_bf[c, g][:].rearrange("p n j -> p (n j)"),
+        def interleave(engine, dst, src):
+            if engine is V:
+                V.tensor_copy(out=dst, in_=src)
+            else:
+                S.copy(out=dst, in_=src)
+
+        def deal_x4():
+            V.tensor_copy(
+                out=x4_codes[:].bitcast(U16),
+                in_=x4_raw[:].bitcast(U16).rearrange("p a (m r) -> p a r m", r=PACK),
             )
-
-        def passes4(c, passes):
-            for a in passes:
-                for r in range(PACK):
-                    if a == 0:
-                        acc[c, r] = psum.tile([P, CH], F32, name="acc%d" % ((c * PACK + r) % 8))
-                    if c < CHUNKS - 1:
-                        moving = w4_early[:, a, 2 * c * CH : 2 * (c + 1) * CH]
-                    else:
-                        moving = w4_late[:, a, :]
-                    nc.tensor.matmul_mx(
-                        out=acc[c, r][:],
-                        lhsT=x4_codes[:, a, r, :].bitcast(FP4X4),
-                        lhsT_scale=x4s[:, a, r, :],
-                        rhs=moving.bitcast(FP4X4),
-                        rhs_scale=w4s[:, a, c * CH : (c + 1) * CH],
-                        start=(a == 0),
-                        stop=False,
-                    )
-
-        def pass8(c, g):
-            for r in range(PACK):
-                nc.tensor.matmul_mx(
-                    out=acc[c, r][:],
-                    lhsT=x8_codes[g][:, r * P : (r + 1) * P].bitcast(FP8X4),
-                    lhsT_scale=x8s[g][:, r * P : (r + 1) * P],
-                    rhs=w8_codes[c, g][:].bitcast(FP8X4),
-                    rhs_scale=w8s[c, g][:],
-                    start=False,
-                    stop=(g == PASSES8 - 1),
-                )
-
-        def rectify(c, r, engine):
-            if engine is nc.vector:
-                nc.vector.tensor_scalar(
-                    out=relu[c][:, r, :], in0=acc[c, r][:], scalar1=0.0, scalar2=None, op0=ALU.max
-                )
-            else:
-                nc.scalar.activation(out=relu[c][:, r, :], in_=acc[c, r][:], func=ACT.Relu)
-
-        def square(c, r, engine):
-            if engine is nc.vector:
-                nc.vector.tensor_tensor(
-                    out=res[c][:, r, :], in0=relu[c][:, r, :], in1=relu[c][:, r, :], op=ALU.mult
-                )
-            else:
-                nc.scalar.activation(out=res[c][:, r, :], in_=relu[c][:, r, :], func=ACT.Square)
-
-        def group_res(c, engine, c0, c1):
-            dst = res_bf[c][:, c0:c1, :].rearrange("p (m i) r -> p m r i", i=PACK)
-            src = res[c][:, :, c0:c1].rearrange("p r (m i) -> p m r i", i=PACK)
-            if engine is nc.vector:
-                nc.vector.tensor_copy(out=dst, in_=src)
-            else:
-                nc.scalar.copy(out=dst, in_=src)
-
-        def quantise_res(c, c0=0, c1=CH):
-            nc.vector.quantize_mx(
-                out=res_codes[:, c * CH + c0 : c * CH + c1].bitcast(FP8X4),
-                scales=res_scales[:, c * CH + c0 : c * CH + c1],
-                in_=res_bf[c][:, c0:c1, :].rearrange("p n r -> p (n r)"),
-            )
-
-        out_rows = out_0.rearrange("(p r) n -> p r n", r=PACK)
-        out_words = out_1[0].rearrange("p n i -> p (n i)").bitcast(I32)
-
-        nc.vector.memset(w4s[:].bitcast(I32), 0)
-        nc.vector.memset(x4s_raw[:].bitcast(I32), 0)
-
-        for r in range(PACK - 1):
-            load_scales(w4s, w4_scales, r, nc.gpsimd)
-        load_words(w4_early, w4_words, 0, 2 * EARLY)
-        load_scales(w4s, w4_scales, PACK - 1, nc.sync)
-        for r in range(PACK):
-            load_scales(x4s_raw, x4_scales, r, nc.sync)
-        load_words(x4_raw, x4_words, 0, 2 * T)
-        for c in range(CHUNKS):
-            if c == CHUNKS - 1:
-                load_words(w4_late, w4_words, 2 * EARLY, 2 * CH)
-            for g in range(PASSES8):
-                if c == 0:
-                    load_rows(x8_raw[g], x8, g, 0, T)
-                load_rows(w8_raw[c, g], w8, g, c * CH, CH)
+            V.tensor_copy(out=x4s[:], in_=x4s_raw[:].rearrange("p a (m r) -> p a r m", r=PACK))
 
         def group_x8(g, engine, m0, m1):
             dst = x8_bf[g][:].rearrange("p (r m j) -> p m j r", r=PACK, j=PACK)[:, m0:m1, :, :]
             src = x8_raw[g][:].rearrange("p j (m r) -> p m j r", r=PACK)[:, m0:m1, :, :]
-            if engine is nc.vector:
-                nc.vector.tensor_copy(out=dst, in_=src)
-            else:
-                nc.scalar.activation(out=dst, in_=src, func=ACT.Copy)
+            interleave(engine, dst, src)
 
         def quantise_x8(g):
-            nc.vector.quantize_mx(
-                out=x8_codes[g][:].bitcast(FP8X4), scales=x8s[g][:], in_=x8_bf[g][:]
+            V.quantize_mx(out=x8_codes[g][:].bitcast(FP8X4), scales=x8s[g][:], in_=x8_bf[g][:])
+
+        def group_w8(h, g, engine, c0, c1):
+            n0 = max(start for start, end in W8_LOADS[g] if start <= PIECES[h][0])
+            at = PIECES[h][0] - n0
+            dst = w8_bf[h, g][:, c0:c1, :].rearrange("p (m i) j -> p m j i", i=PACK)
+            src = w8_raw[g, n0][:, :, at + c0 : at + c1].rearrange("p j (m i) -> p m j i", i=PACK)
+            interleave(engine, dst, src)
+
+        def quantise_w8(h, g):
+            V.quantize_mx(
+                out=w8_codes[h, g][:].bitcast(FP8X4),
+                scales=w8s[h, g][:],
+                in_=w8_bf[h, g][:].rearrange("p n j -> p (n j)"),
             )
 
-        for a in range(PASSES4):
-            nc.vector.tensor_copy(
-                out=x4_codes[:, a, :, :].rearrange("p r (m b) -> p r m b", b=2),
-                in_=x4_raw[:, a, :].rearrange("p (m r b) -> p r m b", r=PACK, b=2),
+        def multiply(h, r, lhsT, lhsT_scale, rhs, rhs_scale, last):
+            rows = BANK // width[h]
+            b = r // rows
+            first = (h, b) not in acc
+            if first:
+                acc[h, b] = psum.tile([P, rows, width[h]], F32, name="acc%d" % ((PIECES[h][0] * PACK // BANK + b) % 8))
+            nc.tensor.matmul_mx(
+                out=acc[h, b][:, r % rows, :],
+                lhsT=lhsT,
+                lhsT_scale=lhsT_scale,
+                rhs=rhs,
+                rhs_scale=rhs_scale,
+                start=first,
+                stop=last and r % rows == rows - 1,
             )
-            nc.vector.tensor_copy(
-                out=x4s[:, a, :, :], in_=x4s_raw[:, a, :].rearrange("p (m r) -> p r m", r=PACK)
-            )
 
-        V, S = nc.vector, nc.scalar
-        scale_rows = out_2[0].rearrange("(q r) n -> r q n", r=PACK)
+        def passes4(h, passes):
+            n0, n1 = PIECES[h]
+            i = max(i for i, (start, end) in enumerate(W4_LOADS) if start <= n0)
+            at = n0 - W4_LOADS[i][0]
+            for a in passes:
+                for r in range(PACK):
+                    multiply(
+                        h,
+                        r,
+                        x4_codes[:, a, r, :].bitcast(FP4X4),
+                        x4s[:, a, r, :],
+                        w4_parts[i][:, a, 2 * at : 2 * (at + n1 - n0)].bitcast(FP4X4),
+                        w4s[:, a, n0:n1],
+                        False,
+                    )
 
-        def prep(c, g, v_cols):
-            if v_cols < CH:
-                group_w8(c, g, S, v_cols, CH)
-            group_w8(c, g, V, 0, v_cols)
-
-        def store_rows(c, r0, r1):
-            nc.sync.dma_start(out=out_rows[:, r0:r1, c * CH : (c + 1) * CH], in_=res[c][:, r0:r1, :])
-
-        def store_words(c0, c1):
-            cols = slice(c0, c1)
-            nc.sync.dma_start(out=out_words[:, cols], in_=res_codes[:, cols].bitcast(I32))
-
-        def store_scales(c0, c1, queue):
-            cols = slice(c0 * CH, c1 * CH)
+        def pass8(h, g):
             for r in range(PACK):
-                queue.dma_start(
-                    out=scale_rows[r][:, cols].bitcast(I32),
-                    in_=res_scales[r:P:32, cols].bitcast(I32),
+                multiply(
+                    h,
+                    r,
+                    x8_codes[g][:, r * P : (r + 1) * P].bitcast(FP8X4),
+                    x8s[g][:, r * P : (r + 1) * P],
+                    w8_codes[h, g][:].bitcast(FP8X4),
+                    w8s[h, g][:],
+                    g == PASSES8 - 1,
                 )
 
-        def finish(c):
-            rectify(c, 0, S)
-            for r in range(PACK):
-                if r + 1 < PACK:
-                    rectify(c, r + 1, S)
-                square(c, r, S)
+        def passes8(h):
+            rows = BANK // width[h]
+            for b in range(PACK // rows):
+                for g in range(PASSES8):
+                    for r in range(b * rows, (b + 1) * rows):
+                        multiply(
+                            h,
+                            r,
+                            x8_codes[g][:, r * P : (r + 1) * P].bitcast(FP8X4),
+                            x8s[g][:, r * P : (r + 1) * P],
+                            w8_codes[h, g][:].bitcast(FP8X4),
+                            w8s[h, g][:],
+                            g == PASSES8 - 1,
+                        )
 
-        passes4(0, range(PASSES4))
+        def result(h):
+            n0, n1 = PIECES[h]
+            i = max(i for i, (start, end) in enumerate(STORES) if start <= n0)
+            return res[i][:, :, n0 - STORES[i][0] : n1 - STORES[i][0]]
+
+        def bank_rows(h, b):
+            rows = BANK // width[h]
+            return slice(b * rows, (b + 1) * rows)
+
+        def rectify(h, b, engine):
+            dst = relu[h][:, bank_rows(h, b), :]
+            if engine is V:
+                V.tensor_scalar(out=dst, in0=acc[h, b][:], scalar1=0.0, scalar2=None, op0=ALU.max)
+            else:
+                S.activation(out=dst, in_=acc[h, b][:], func=ACT.Relu)
+
+        def square(h, b, engine):
+            src = relu[h][:, bank_rows(h, b), :]
+            dst = result(h)[:, bank_rows(h, b), :]
+            if engine is V:
+                V.tensor_tensor(out=dst, in0=src, in1=src, op=ALU.mult)
+            else:
+                S.activation(out=dst, in_=src, func=ACT.Square)
+
+        def group_res(h, engine, c0, c1):
+            dst = res_bf[h][:, c0:c1, :].rearrange("p (m i) r -> p m r i", i=PACK)
+            src = result(h)[:, :, c0:c1].rearrange("p r (m i) -> p m r i", i=PACK)
+            interleave(engine, dst, src)
+
+        def quantise_res(h):
+            cols = slice(PIECES[h][0], PIECES[h][1])
+            V.quantize_mx(
+                out=res_codes[:, cols].bitcast(FP8X4),
+                scales=res_scales[:, cols],
+                in_=res_bf[h][:].rearrange("p n r -> p (n r)"),
+            )
+
+        def store_rows(i, r0, r1):
+            n0, n1 = STORES[i]
+            nc.sync.dma_start(out=out_rows[:, r0:r1, n0:n1], in_=res[i][:, r0:r1, :])
+
+        def store_words(n0, n1):
+            nc.sync.dma_start(out=out_words[:, n0:n1], in_=res_codes[:, n0:n1].bitcast(I32))
+
+        def store_scales(n0, n1, queue):
+            for r in range(PACK):
+                queue.dma_start(
+                    out=scale_rows[r][:, n0:n1].bitcast(I32),
+                    in_=res_scales[r:P:32, n0:n1].bitcast(I32),
+                )
+
+        V.memset(w4s[:].bitcast(I32), 0)
+        V.memset(x4s_raw[:].bitcast(I32), 0)
+
+        for r in range(PACK):
+            load_scales(w4s, w4_scales, r, nc.gpsimd)
+        load_x8(0)
+        load_words(x4_raw, x4_words, 0, T)
+        for r in range(PACK):
+            load_scales(x4s_raw, x4_scales, r, nc.sync)
+        load_x8(1)
+        for c in range(3):
+            load_w4(c)
+            load_w8(0, c)
+            load_w8(1, 2 * c)
+            load_w8(1, 2 * c + 1)
+
+        def prepare(c, helper):
+            a, b = 2 * c, 2 * c + 1
+            passes4(a, range(PASSES4))
+            passes4(b, range(PASSES4))
+            group_w8(a, 0, V, 0, 256)
+            group_w8(b, 0, helper, 0, 256)
+            group_w8(a, 1, V, 0, 256)
+            quantise_w8(a, 0)
+            quantise_w8(a, 1)
+            passes8(a)
+            group_w8(b, 1, V, 0, 256)
+            quantise_w8(b, 0)
+            quantise_w8(b, 1)
+            passes8(b)
+
+        def finish(h):
+            rectify(h, 0, S)
+            rectify(h, 1, S)
+            square(h, 0, S)
+            square(h, 1, S)
+
         group_x8(0, S, 0, P)
-        prep(0, 0, 256)
+        deal_x4()
         quantise_x8(0)
-        quantise_w8(0, 0)
-        pass8(0, 0)
-        passes4(1, [0])
         group_x8(1, S, 64, P)
         group_x8(1, V, 0, 64)
         quantise_x8(1)
-        prep(0, 1, 352)
-        quantise_w8(0, 1)
-        pass8(0, 1)
-        passes4(1, [1, 2])
-        for r in range(PACK):
-            rectify(0, r, S)
-        group_w8(1, 0, V, 0, CH)
 
-        quantise_w8(1, 0)
-        pass8(1, 0)
-        square(0, 0, S)
-        prep(1, 1, 512)
-        quantise_w8(1, 1)
-        pass8(1, 1)
-        square(0, 1, S)
-        square(0, 2, S)
-        square(0, 3, S)
-        store_rows(0, 0, PACK)
-        passes4(2, range(PASSES4))
-        group_res(0, S, 384, CH)
-        group_res(0, V, 0, 384)
-        for r in range(PACK):
-            rectify(1, r, S)
-        group_w8(2, 0, V, 0, CH)
-        quantise_res(0)
-        quantise_w8(2, 0)
-        pass8(2, 0)
+        prepare(0, S)
+        finish(0)
+        rectify(1, 0, V)
+        rectify(1, 1, S)
         square(1, 0, S)
         square(1, 1, S)
-        store_rows(1, 0, 2)
-        square(1, 2, S)
-        square(1, 3, S)
-        prep(2, 1, 512)
-        quantise_w8(2, 1)
-        pass8(2, 1)
+        store_rows(0, 0, PACK)
+        group_res(0, S, 0, 256)
 
-        store_rows(1, 2, PACK)
-        store_words(0, CH)
-        group_res(1, S, 256, CH)
+        prepare(1, V)
         group_res(1, V, 0, 256)
-        rectify(2, 0, S)
+        quantise_res(0)
         quantise_res(1)
-        store_words(CH, 2 * CH)
-        rectify(2, 1, S)
-        square(2, 0, V)
-        store_rows(2, 0, 1)
-        rectify(2, 2, S)
-        rectify(2, 3, V)
-        square(2, 1, S)
-        store_rows(2, 1, 2)
-        square(2, 2, V)
-        store_rows(2, 2, 3)
-        square(2, 3, S)
-        store_rows(2, 3, 4)
-        group_res(2, S, 352, CH)
-        group_res(2, V, 0, CH // 2)
-        group_res(2, V, CH // 2, 352)
-        quantise_res(2, 0, CH // 2)
-        store_words(2 * CH, 2 * CH + CH // 2)
-        quantise_res(2, CH // 2, CH)
-        store_words(2 * CH + CH // 2, N)
-        store_scales(0, 3, nc.scalar)
+        store_words(0, 512)
+        finish(2)
+        rectify(3, 0, S)
+        rectify(3, 1, S)
+        square(3, 0, S)
+        store_rows(1, 0, 2)
+        square(3, 1, S)
+        store_rows(1, 2, 4)
+        group_res(2, S, 0, 256)
+
+        prepare(2, V)
+        group_res(3, V, 0, 256)
+        quantise_res(2)
+        finish(4)
+        quantise_res(3)
+        rectify(5, 0, V)
+        store_words(512, 1024)
+        rectify(5, 1, V)
+        square(5, 0, S)
+        store_rows(2, 0, 2)
+        square(5, 1, S)
+        store_rows(2, 2, 4)
+        group_res(4, V, 0, 256)
+        quantise_res(4)
+        group_res(5, S, 176, 256)
+        group_res(5, V, 0, 176)
+        quantise_res(5)
+        store_scales(0, N, nc.scalar)
+        store_words(1024, N)

@@ -23,9 +23,10 @@ PASSES8 = O // K_PASS
 PASSES4 = K4 // K_PASS
 BANK = 512
 PIECES = [(n, n + 256) for n in range(0, N, 256)]
-W4_LOADS = [(n, n + 512) for n in range(0, N, 512)]
-W8_LOADS = [W4_LOADS, PIECES]
-STORES = W4_LOADS
+CHUNKS = [(n, n + 512) for n in range(0, N, 512)]
+STORES = CHUNKS
+W4_LOADS = [(0, 1024), (1024, 1536)]
+W8_LOADS = [CHUNKS, CHUNKS[:1] + PIECES[2:]]
 
 
 def tile_mix_atom_tm_pl_relu2_kernel(
@@ -219,12 +220,13 @@ def tile_mix_atom_tm_pl_relu2_kernel(
             src = result(h)[:, :, c0:c1].rearrange("p r (m i) -> p m r i", i=PACK)
             interleave(engine, dst, src)
 
-        def quantise_res(h):
-            cols = slice(PIECES[h][0], PIECES[h][1])
+        def quantise_res(h, c0=0, c1=None):
+            c1 = width[h] if c1 is None else c1
+            cols = slice(PIECES[h][0] + c0, PIECES[h][0] + c1)
             V.quantize_mx(
                 out=res_codes[:, cols].bitcast(FP8X4),
                 scales=res_scales[:, cols],
-                in_=res_bf[h][:].rearrange("p n r -> p (n r)"),
+                in_=res_bf[h][:, c0:c1, :].rearrange("p n r -> p (n r)"),
             )
 
         def store_rows(i, r0, r1):
@@ -250,27 +252,17 @@ def tile_mix_atom_tm_pl_relu2_kernel(
         load_words(x4_raw, x4_words, 0, T)
         for r in range(PACK):
             load_scales(x4s_raw, x4_scales, r, nc.sync)
+        load_w4(0)
         load_x8(1)
-        for c in range(3):
-            load_w4(c)
-            load_w8(0, c)
-            load_w8(1, 2 * c)
-            load_w8(1, 2 * c + 1)
-
-        def prepare(c, helper):
-            a, b = 2 * c, 2 * c + 1
-            passes4(a, range(PASSES4))
-            passes4(b, range(PASSES4))
-            group_w8(a, 0, V, 0, 256)
-            group_w8(b, 0, helper, 0, 256)
-            group_w8(a, 1, V, 0, 256)
-            quantise_w8(a, 0)
-            quantise_w8(a, 1)
-            passes8(a)
-            group_w8(b, 1, V, 0, 256)
-            quantise_w8(b, 0)
-            quantise_w8(b, 1)
-            passes8(b)
+        load_w8(0, 0)
+        load_w8(1, 0)
+        load_w8(0, 1)
+        load_w8(1, 1)
+        load_w8(1, 2)
+        load_w4(1)
+        load_w8(0, 2)
+        load_w8(1, 3)
+        load_w8(1, 4)
 
         def finish(h):
             rectify(h, 0, S)
@@ -281,20 +273,47 @@ def tile_mix_atom_tm_pl_relu2_kernel(
         group_x8(0, S, 0, P)
         deal_x4()
         quantise_x8(0)
-        group_x8(1, S, 64, P)
-        group_x8(1, V, 0, 64)
+        group_x8(1, S, 80, P)
+        group_x8(1, V, 0, 80)
         quantise_x8(1)
-
-        prepare(0, S)
+        passes4(0, range(PASSES4))
+        passes4(1, range(PASSES4))
+        passes4(2, range(2))
+        group_w8(0, 0, V, 0, 256)
+        group_w8(1, 0, S, 0, 256)
+        quantise_w8(0, 0)
+        quantise_w8(1, 0)
+        pass8(0, 0)
+        pass8(1, 0)
+        group_w8(0, 1, V, 0, 256)
+        group_w8(1, 1, S, 128, 256)
+        group_w8(1, 1, V, 0, 128)
+        quantise_w8(0, 1)
+        pass8(0, 1)
+        quantise_w8(1, 1)
+        pass8(1, 1)
+        passes4(2, range(2, PASSES4))
+        passes4(3, range(PASSES4))
         finish(0)
-        rectify(1, 0, V)
+        rectify(1, 0, S)
         rectify(1, 1, S)
         square(1, 0, S)
         square(1, 1, S)
         store_rows(0, 0, PACK)
-        group_res(0, S, 0, 256)
 
-        prepare(1, V)
+        group_w8(2, 0, V, 0, 256)
+        group_w8(3, 0, V, 0, 256)
+        group_w8(2, 1, V, 0, 256)
+        quantise_w8(2, 0)
+        quantise_w8(2, 1)
+        passes8(2)
+        group_w8(3, 1, V, 0, 256)
+        quantise_w8(3, 0)
+        quantise_w8(3, 1)
+        passes8(3)
+        passes4(4, range(PASSES4))
+        passes4(5, range(PASSES4))
+        group_res(0, V, 0, 256)
         group_res(1, V, 0, 256)
         quantise_res(0)
         quantise_res(1)
@@ -307,23 +326,33 @@ def tile_mix_atom_tm_pl_relu2_kernel(
         square(3, 1, S)
         store_rows(1, 2, 4)
         group_res(2, S, 0, 256)
+        group_res(3, S, 128, 256)
 
-        prepare(2, V)
-        group_res(3, V, 0, 256)
+        group_w8(4, 0, V, 0, 256)
+        group_w8(5, 0, V, 0, 256)
+        group_w8(4, 1, V, 0, 256)
+        quantise_w8(4, 0)
+        quantise_w8(4, 1)
+        passes8(4)
+        group_w8(5, 1, V, 0, 256)
+        quantise_w8(5, 0)
+        quantise_w8(5, 1)
+        passes8(5)
+        group_res(3, V, 0, 128)
         quantise_res(2)
-        finish(4)
         quantise_res(3)
-        rectify(5, 0, V)
         store_words(512, 1024)
+        finish(4)
+        rectify(5, 0, V)
         rectify(5, 1, V)
-        square(5, 0, S)
+        square(5, 0, V)
         store_rows(2, 0, 2)
         square(5, 1, S)
         store_rows(2, 2, 4)
         group_res(4, V, 0, 256)
-        quantise_res(4)
         group_res(5, S, 176, 256)
         group_res(5, V, 0, 176)
+        quantise_res(4)
         quantise_res(5)
         store_scales(0, N, nc.scalar)
         store_words(1024, N)

@@ -25,6 +25,7 @@ BANK = 512
 PIECES = [(n, n + 256) for n in range(0, N, 256)]
 CHUNKS = [(n, n + 512) for n in range(0, N, 512)]
 STORES = CHUNKS
+PLANE = 4
 W4_LOADS = [(0, 1024), (1024, 1536)]
 W8_LOADS = [CHUNKS, CHUNKS[:1] + PIECES[2:]]
 
@@ -225,7 +226,7 @@ def tile_mix_atom_tm_pl_relu2_kernel(
             cols = slice(PIECES[h][0] + c0, PIECES[h][0] + c1)
             V.quantize_mx(
                 out=res_codes[:, cols].bitcast(FP8X4),
-                scales=res_scales[:, cols],
+                scales=res_scales[PLANE:P, cols],
                 in_=res_bf[h][:, c0:c1, :].rearrange("p n r -> p (n r)"),
             )
 
@@ -240,7 +241,7 @@ def tile_mix_atom_tm_pl_relu2_kernel(
             for r in range(PACK):
                 queue.dma_start(
                     out=scale_rows[r][:, n0:n1].bitcast(I32),
-                    in_=res_scales[r:P:32, n0:n1].bitcast(I32),
+                    in_=res_scales[PLANE + r : P : 32, n0:n1].bitcast(I32),
                 )
 
         V.memset(w4s[:].bitcast(I32), 0)

@@ -27,7 +27,7 @@ CHUNKS = [(n, n + 512) for n in range(0, N, 512)]
 STORES = CHUNKS
 PLANE = 4
 W4_LOADS = [(0, 1024), (1024, 1536)]
-W8_LOADS = [CHUNKS, CHUNKS[:1] + PIECES[2:]]
+W8_LOADS = [CHUNKS, PIECES]
 
 
 def tile_mix_atom_tm_pl_relu2_kernel(
@@ -105,11 +105,13 @@ def tile_mix_atom_tm_pl_relu2_kernel(
                 S.copy(out=dst, in_=src)
 
         def deal_x4():
-            V.tensor_copy(
-                out=x4_codes[:].bitcast(U16),
-                in_=x4_raw[:].bitcast(U16).rearrange("p a (m r) -> p a r m", r=PACK),
-            )
-            V.tensor_copy(out=x4s[:], in_=x4s_raw[:].rearrange("p a (m r) -> p a r m", r=PACK))
+            for a in range(PASSES4):
+                V.tensor_copy(
+                    out=x4_codes[:, a, :, :].bitcast(U16),
+                    in_=x4_raw[:, a, :].bitcast(U16).rearrange("p (m r) -> p r m", r=PACK),
+                )
+            for a in range(PASSES4):
+                V.tensor_copy(out=x4s[:, a, :, :], in_=x4s_raw[:, a, :].rearrange("p (m r) -> p r m", r=PACK))
 
         def group_x8(g, engine, m0, m1):
             dst = x8_bf[g][:].rearrange("p (r m j) -> p m j r", r=PACK, j=PACK)[:, m0:m1, :, :]
@@ -257,13 +259,14 @@ def tile_mix_atom_tm_pl_relu2_kernel(
         load_x8(1)
         load_w8(0, 0)
         load_w8(1, 0)
-        load_w8(0, 1)
         load_w8(1, 1)
+        load_w8(0, 1)
         load_w8(1, 2)
+        load_w8(1, 3)
         load_w4(1)
         load_w8(0, 2)
-        load_w8(1, 3)
         load_w8(1, 4)
+        load_w8(1, 5)
 
         def finish(h):
             rectify(h, 0, S)
@@ -279,27 +282,22 @@ def tile_mix_atom_tm_pl_relu2_kernel(
         quantise_x8(1)
         passes4(0, range(PASSES4))
         passes4(1, range(PASSES4))
-        passes4(2, range(2))
+        passes4(2, range(3))
         group_w8(0, 0, V, 0, 256)
         group_w8(1, 0, S, 0, 256)
         quantise_w8(0, 0)
-        quantise_w8(1, 0)
         pass8(0, 0)
-        pass8(1, 0)
         group_w8(0, 1, V, 0, 256)
-        group_w8(1, 1, S, 128, 256)
-        group_w8(1, 1, V, 0, 128)
+        quantise_w8(1, 0)
         quantise_w8(0, 1)
         pass8(0, 1)
+        pass8(1, 0)
+        group_w8(1, 1, V, 0, 256)
         quantise_w8(1, 1)
         pass8(1, 1)
-        passes4(2, range(2, PASSES4))
         passes4(3, range(PASSES4))
         finish(0)
-        rectify(1, 0, S)
-        rectify(1, 1, S)
-        square(1, 0, S)
-        square(1, 1, S)
+        finish(1)
         store_rows(0, 0, PACK)
 
         group_w8(2, 0, V, 0, 256)

@@ -41,7 +41,7 @@ def tile_mix_atom_tm_pl_relu2_kernel(
         V, S = nc.vector, nc.scalar
 
         def tile(name, shape, dtype):
-            return sb.tile(shape, dtype, name=name, align_bytes=64)
+            return sb.tile(shape, dtype, name=name, align_bytes=256)
 
         x4_raw = tile("x4_raw", [P, PASSES4, 2 * T], U8)
         x4_codes = tile("x4_codes", [P, PASSES4, PACK, 2 * P], U8)

@@ -29,7 +29,6 @@ PLANE = 4
 W4_LOADS = [(0, 1024), (1024, 1536)]
 W8_LOADS = [CHUNKS, PIECES]
 
-
 def tile_mix_atom_tm_pl_relu2_kernel(
     tc, x8, w8, x4_words, x4_scales, w4_words, w4_scales, out_0, out_1, out_2
 ):
@@ -106,12 +105,11 @@ def tile_mix_atom_tm_pl_relu2_kernel(
 
         def deal_x4():
             for a in range(PASSES4):
+                V.tensor_copy(out=x4s[:, a, :, :], in_=x4s_raw[:, a, :].rearrange("p (m r) -> p r m", r=PACK))
                 V.tensor_copy(
                     out=x4_codes[:, a, :, :].bitcast(U16),
                     in_=x4_raw[:, a, :].bitcast(U16).rearrange("p (m r) -> p r m", r=PACK),
                 )
-            for a in range(PASSES4):
-                V.tensor_copy(out=x4s[:, a, :, :], in_=x4s_raw[:, a, :].rearrange("p (m r) -> p r m", r=PACK))
 
         def group_x8(g, engine, m0, m1):
             dst = x8_bf[g][:].rearrange("p (r m j) -> p m j r", r=PACK, j=PACK)[:, m0:m1, :, :]
@@ -249,13 +247,15 @@ def tile_mix_atom_tm_pl_relu2_kernel(
         V.memset(w4s[:].bitcast(I32), 0)
         V.memset(x4s_raw[:].bitcast(I32), 0)
 
-        for r in range(PACK):
+        for r in range(2):
             load_scales(w4s, w4_scales, r, nc.gpsimd)
-        load_x8(0)
         load_words(x4_raw, x4_words, 0, T)
+        load_w4(0)
         for r in range(PACK):
             load_scales(x4s_raw, x4_scales, r, nc.sync)
-        load_w4(0)
+        for r in range(2, PACK):
+            load_scales(w4s, w4_scales, r, nc.sync)
+        load_x8(0)
         load_x8(1)
         load_w8(0, 0)
         load_w8(1, 0)
@@ -274,15 +274,16 @@ def tile_mix_atom_tm_pl_relu2_kernel(
             square(h, 0, S)
             square(h, 1, S)
 
-        group_x8(0, S, 0, P)
         deal_x4()
+        group_x8(0, S, 80, P)
+        group_x8(0, V, 0, 80)
         quantise_x8(0)
         group_x8(1, S, 80, P)
         group_x8(1, V, 0, 80)
         quantise_x8(1)
         passes4(0, range(PASSES4))
         passes4(1, range(PASSES4))
-        passes4(2, range(3))
+        passes4(2, range(PASSES4))
         group_w8(0, 0, V, 0, 256)
         group_w8(1, 0, S, 0, 256)
         quantise_w8(0, 0)

@@ -24,7 +24,7 @@ PASSES4 = K4 // K_PASS
 BANK = 512
 PIECES = [(n, n + 256) for n in range(0, N, 256)]
 CHUNKS = [(n, n + 512) for n in range(0, N, 512)]
-STORES = CHUNKS
+STORES = CHUNKS[:2] + PIECES[4:]
 PLANE = 4
 W4_LOADS = [(0, 1024), (1024, 1536)]
 W8_LOADS = [CHUNKS, PIECES]
@@ -312,7 +312,7 @@ def tile_mix_atom_tm_pl_relu2_kernel(
         quantise_w8(3, 1)
         passes8(3)
         passes4(4, range(PASSES4))
-        passes4(5, range(PASSES4))
+        passes4(5, range(2))
         group_res(0, V, 0, 256)
         group_res(1, V, 0, 256)
         quantise_res(0)
@@ -326,7 +326,6 @@ def tile_mix_atom_tm_pl_relu2_kernel(
         square(3, 1, S)
         store_rows(1, 2, 4)
         group_res(2, S, 0, 256)
-        group_res(3, S, 128, 256)
 
         group_w8(4, 0, V, 0, 256)
         group_w8(5, 0, V, 0, 256)
@@ -334,22 +333,24 @@ def tile_mix_atom_tm_pl_relu2_kernel(
         quantise_w8(4, 0)
         quantise_w8(4, 1)
         passes8(4)
+        passes4(5, range(2, PASSES4))
         group_w8(5, 1, V, 0, 256)
         quantise_w8(5, 0)
         quantise_w8(5, 1)
         passes8(5)
-        group_res(3, V, 0, 128)
+        group_res(3, V, 0, 256)
         quantise_res(2)
         quantise_res(3)
         store_words(512, 1024)
         finish(4)
+        store_rows(2, 0, PACK)
         rectify(5, 0, V)
-        rectify(5, 1, V)
+        rectify(5, 1, S)
+        group_res(4, V, 0, 128)
         square(5, 0, V)
-        store_rows(2, 0, 2)
         square(5, 1, S)
-        store_rows(2, 2, 4)
-        group_res(4, V, 0, 256)
+        store_rows(3, 0, PACK)
+        group_res(4, V, 128, 256)
         group_res(5, S, 176, 256)
         group_res(5, V, 0, 176)
         quantise_res(4)

@@ -22,12 +22,23 @@ K_PASS = P * PACK
 PASSES8 = O // K_PASS
 PASSES4 = K4 // K_PASS
 BANK = 512
-PIECES = [(n, n + 256) for n in range(0, N, 256)]
-CHUNKS = [(n, n + 512) for n in range(0, N, 512)]
-STORES = CHUNKS[:2] + PIECES[4:]
+BANKS = 8
 PLANE = 4
-W4_LOADS = [(0, 1024), (1024, 1536)]
-W8_LOADS = [CHUNKS, PIECES]
+
+
+def spans(*edges):
+    return list(zip(edges[:-1], edges[1:]))
+
+
+PIECES = spans(0, 256, 512, 768, 1024, 1280, 1536)
+STORES = spans(0, 512, 1024, 1280, 1536)
+W4_LOADS = spans(0, 1280, 1536)
+W8_LOADS = [spans(0, 512, 1024, 1280, 1536), PIECES]
+
+
+def holder(table, n):
+    return max(i for i, (n0, n1) in enumerate(table) if n0 <= n)
+
 
 def tile_mix_atom_tm_pl_relu2_kernel(
     tc, x8, w8, x4_words, x4_scales, w4_words, w4_scales, out_0, out_1, out_2
@@ -46,30 +57,26 @@ def tile_mix_atom_tm_pl_relu2_kernel(
         x4_codes = tile("x4_codes", [P, PASSES4, PACK, 2 * P], U8)
         x4s_raw = tile("x4s_raw", [P, PASSES4, T], U8)
         x4s = tile("x4s", [P, PASSES4, PACK, P], U8)
-        w4_parts = [
-            tile("w4_part%d" % i, [P, PASSES4, 2 * (n1 - n0)], U8) for i, (n0, n1) in enumerate(W4_LOADS)
-        ]
+        w4_parts = [tile("w4_part%d" % i, [P, PASSES4, 2 * (n1 - n0)], U8) for i, (n0, n1) in enumerate(W4_LOADS)]
         w4s = tile("w4s", [P, PASSES4, N], U8)
         x8_raw = [tile("x8_raw%d" % g, [P, PACK, T], F32) for g in range(PASSES8)]
         x8_bf = [tile("x8_bf%d" % g, [P, T * PACK], BF16) for g in range(PASSES8)]
         x8_codes = [tile("x8_codes%d" % g, [P, T], U32) for g in range(PASSES8)]
         x8s = [tile("x8s%d" % g, [P, T], U8) for g in range(PASSES8)]
-        w8_raw = {
-            (g, n0): tile("w8_raw%d_%d" % (g, n0), [P, PACK, n1 - n0], F32)
-            for g in range(PASSES8)
-            for n0, n1 in W8_LOADS[g]
-        }
+        w8_raw = [
+            [tile("w8_raw%d_%d" % (g, n0), [P, PACK, n1 - n0], F32) for n0, n1 in W8_LOADS[g]] for g in range(PASSES8)
+        ]
+        w8_bf = [tile("w8_bf%d" % g, [P, N * PACK], BF16) for g in range(PASSES8)]
+        w8_codes = [tile("w8_codes%d" % g, [P, N], U32) for g in range(PASSES8)]
+        w8s = [tile("w8s%d" % g, [P, N], U8) for g in range(PASSES8)]
         width = [n1 - n0 for n0, n1 in PIECES]
-        keys = [(h, g) for h in range(len(PIECES)) for g in range(PASSES8)]
-        w8_bf = {k: tile("w8_bf%d_%d" % k, [P, width[k[0]], PACK], BF16) for k in keys}
-        w8_codes = {k: tile("w8_codes%d_%d" % k, [P, width[k[0]]], U32) for k in keys}
-        w8s = {k: tile("w8s%d_%d" % k, [P, width[k[0]]], U8) for k in keys}
         relu = [tile("relu%d" % h, [P, PACK, w], F32) for h, w in enumerate(width)]
         res = [tile("res%d" % i, [P, PACK, n1 - n0], F32) for i, (n0, n1) in enumerate(STORES)]
-        res_bf = [tile("res_bf%d" % h, [P, w, PACK], BF16) for h, w in enumerate(width)]
+        res_bf = tile("res_bf", [P, N * PACK], BF16)
         res_codes = tile("res_codes", [P, N], U32)
         res_scales = tile("res_scales", [P, N], U8)
         acc = {}
+        done = {}
 
         out_rows = out_0.rearrange("(p r) n -> p r n", r=PACK)
         out_words = out_1[0].rearrange("p n i -> p (n i)").bitcast(I32)
@@ -87,15 +94,14 @@ def tile_mix_atom_tm_pl_relu2_kernel(
             load_rows(x8_raw[g], x8, g, 0, T)
 
         def load_w8(g, i):
-            n0, n1 = W8_LOADS[g][i]
-            load_rows(w8_raw[g, n0], w8, g, n0, n1)
+            load_rows(w8_raw[g][i], w8, g, *W8_LOADS[g][i])
 
         def load_words(dst, src, n0, n1):
             words = src[:, :, 2 * n0 : 2 * n1].rearrange("a p w -> p a w")
             nc.sync.dma_start(out=dst[:].bitcast(I32), in_=words.bitcast(I32))
 
         def load_w4(i):
-            load_words(w4_parts[i], w4_words, W4_LOADS[i][0], W4_LOADS[i][1])
+            load_words(w4_parts[i], w4_words, *W4_LOADS[i])
 
         def interleave(engine, dst, src):
             if engine is V:
@@ -103,13 +109,19 @@ def tile_mix_atom_tm_pl_relu2_kernel(
             else:
                 S.copy(out=dst, in_=src)
 
-        def deal_x4():
-            for a in range(PASSES4):
-                V.tensor_copy(out=x4s[:, a, :, :], in_=x4s_raw[:, a, :].rearrange("p (m r) -> p r m", r=PACK))
-                V.tensor_copy(
-                    out=x4_codes[:, a, :, :].bitcast(U16),
-                    in_=x4_raw[:, a, :].bitcast(U16).rearrange("p (m r) -> p r m", r=PACK),
-                )
+        def deal_x4(a):
+            V.tensor_copy(out=x4s[:, a, :, :], in_=x4s_raw[:, a, :].rearrange("p (m r) -> p r m", r=PACK))
+            deal_words(a, V)
+
+        def deal_scales(a):
+            V.tensor_copy(out=x4s[:, a, :, :], in_=x4s_raw[:, a, :].rearrange("p (m r) -> p r m", r=PACK))
+
+        def deal_words(a, engine):
+            interleave(
+                engine,
+                x4_codes[:, a, :, :].bitcast(U16),
+                x4_raw[:, a, :].bitcast(U16).rearrange("p (m r) -> p r m", r=PACK),
+            )
 
         def group_x8(g, engine, m0, m1):
             dst = x8_bf[g][:].rearrange("p (r m j) -> p m j r", r=PACK, j=PACK)[:, m0:m1, :, :]
@@ -119,82 +131,81 @@ def tile_mix_atom_tm_pl_relu2_kernel(
         def quantise_x8(g):
             V.quantize_mx(out=x8_codes[g][:].bitcast(FP8X4), scales=x8s[g][:], in_=x8_bf[g][:])
 
-        def group_w8(h, g, engine, c0, c1):
-            n0 = max(start for start, end in W8_LOADS[g] if start <= PIECES[h][0])
-            at = PIECES[h][0] - n0
-            dst = w8_bf[h, g][:, c0:c1, :].rearrange("p (m i) j -> p m j i", i=PACK)
-            src = w8_raw[g, n0][:, :, at + c0 : at + c1].rearrange("p j (m i) -> p m j i", i=PACK)
+        def group_w8(g, engine, n0, n1):
+            i = holder(W8_LOADS[g], n0)
+            at = W8_LOADS[g][i][0]
+            dst = w8_bf[g][:, PACK * n0 : PACK * n1].rearrange("p (m i j) -> p m j i", i=PACK, j=PACK)
+            src = w8_raw[g][i][:, :, n0 - at : n1 - at].rearrange("p j (m i) -> p m j i", i=PACK)
             interleave(engine, dst, src)
 
-        def quantise_w8(h, g):
+        def quantise_w8(g, n0, n1):
             V.quantize_mx(
-                out=w8_codes[h, g][:].bitcast(FP8X4),
-                scales=w8s[h, g][:],
-                in_=w8_bf[h, g][:].rearrange("p n j -> p (n j)"),
+                out=w8_codes[g][:, n0:n1].bitcast(FP8X4),
+                scales=w8s[g][:, n0:n1],
+                in_=w8_bf[g][:, PACK * n0 : PACK * n1],
             )
 
-        def multiply(h, r, lhsT, lhsT_scale, rhs, rhs_scale, last):
+        def multiply(h, r, lhsT, lhsT_scale, rhs, rhs_scale, c0, c1):
             rows = BANK // width[h]
             b = r // rows
             first = (h, b) not in acc
             if first:
-                acc[h, b] = psum.tile([P, rows, width[h]], F32, name="acc%d" % ((PIECES[h][0] * PACK // BANK + b) % 8))
+                acc[h, b] = psum.tile([P, rows, width[h]], F32, name="acc%d" % (len(acc) % BANKS))
+                done[h, b] = 0
+            done[h, b] = done[h, b] + c1 - c0
             nc.tensor.matmul_mx(
-                out=acc[h, b][:, r % rows, :],
+                out=acc[h, b][:, r % rows, c0:c1],
                 lhsT=lhsT,
                 lhsT_scale=lhsT_scale,
                 rhs=rhs,
                 rhs_scale=rhs_scale,
                 start=first,
-                stop=last and r % rows == rows - 1,
+                stop=done[h, b] == (PASSES4 + PASSES8) * BANK,
             )
 
-        def passes4(h, passes):
+        def pass4(h, a, token_rows=range(PACK)):
             n0, n1 = PIECES[h]
-            i = max(i for i, (start, end) in enumerate(W4_LOADS) if start <= n0)
-            at = n0 - W4_LOADS[i][0]
-            for a in passes:
-                for r in range(PACK):
-                    multiply(
-                        h,
-                        r,
-                        x4_codes[:, a, r, :].bitcast(FP4X4),
-                        x4s[:, a, r, :],
-                        w4_parts[i][:, a, 2 * at : 2 * (at + n1 - n0)].bitcast(FP4X4),
-                        w4s[:, a, n0:n1],
-                        False,
-                    )
+            i = holder(W4_LOADS, n0)
+            at = W4_LOADS[i][0]
+            for r in token_rows:
+                multiply(
+                    h,
+                    r,
+                    x4_codes[:, a, r, :].bitcast(FP4X4),
+                    x4s[:, a, r, :],
+                    w4_parts[i][:, a, 2 * (n0 - at) : 2 * (n1 - at)].bitcast(FP4X4),
+                    w4s[:, a, n0:n1],
+                    0,
+                    n1 - n0,
+                )
 
-        def pass8(h, g):
-            for r in range(PACK):
+        def passes4(h):
+            for a in range(PASSES4):
+                pass4(h, a)
+
+        def pass8(h, g, token_rows=range(PACK), c0=0, c1=None):
+            n0, n1 = PIECES[h]
+            c1 = n1 - n0 if c1 is None else c1
+            for r in token_rows:
                 multiply(
                     h,
                     r,
                     x8_codes[g][:, r * P : (r + 1) * P].bitcast(FP8X4),
                     x8s[g][:, r * P : (r + 1) * P],
-                    w8_codes[h, g][:].bitcast(FP8X4),
-                    w8s[h, g][:],
-                    g == PASSES8 - 1,
+                    w8_codes[g][:, n0 + c0 : n0 + c1].bitcast(FP8X4),
+                    w8s[g][:, n0 + c0 : n0 + c1],
+                    c0,
+                    c1,
                 )
 
-        def passes8(h):
+        def both8(h):
             rows = BANK // width[h]
-            for b in range(PACK // rows):
+            for r in range(0, PACK, rows):
                 for g in range(PASSES8):
-                    for r in range(b * rows, (b + 1) * rows):
-                        multiply(
-                            h,
-                            r,
-                            x8_codes[g][:, r * P : (r + 1) * P].bitcast(FP8X4),
-                            x8s[g][:, r * P : (r + 1) * P],
-                            w8_codes[h, g][:].bitcast(FP8X4),
-                            w8s[h, g][:],
-                            g == PASSES8 - 1,
-                        )
+                    pass8(h, g, range(r, r + rows))
 
-        def result(h):
-            n0, n1 = PIECES[h]
-            i = max(i for i, (start, end) in enumerate(STORES) if start <= n0)
+        def result(n0, n1):
+            i = holder(STORES, n0)
             return res[i][:, :, n0 - STORES[i][0] : n1 - STORES[i][0]]
 
         def bank_rows(h, b):
@@ -210,43 +221,47 @@ def tile_mix_atom_tm_pl_relu2_kernel(
 
         def square(h, b, engine):
             src = relu[h][:, bank_rows(h, b), :]
-            dst = result(h)[:, bank_rows(h, b), :]
+            dst = result(*PIECES[h])[:, bank_rows(h, b), :]
             if engine is V:
                 V.tensor_tensor(out=dst, in0=src, in1=src, op=ALU.mult)
             else:
                 S.activation(out=dst, in_=src, func=ACT.Square)
 
-        def group_res(h, engine, c0, c1):
-            dst = res_bf[h][:, c0:c1, :].rearrange("p (m i) r -> p m r i", i=PACK)
-            src = result(h)[:, :, c0:c1].rearrange("p r (m i) -> p m r i", i=PACK)
+        def finish(h, engine=S):
+            banks = range(PACK * width[h] // BANK)
+            for b in banks:
+                rectify(h, b, engine)
+            for b in banks:
+                square(h, b, engine)
+
+        def group_res(engine, n0, n1):
+            dst = res_bf[:, PACK * n0 : PACK * n1].rearrange("p (m i r) -> p m r i", i=PACK, r=PACK)
+            src = result(n0, n1).rearrange("p r (m i) -> p m r i", i=PACK)
             interleave(engine, dst, src)
 
-        def quantise_res(h, c0=0, c1=None):
-            c1 = width[h] if c1 is None else c1
-            cols = slice(PIECES[h][0] + c0, PIECES[h][0] + c1)
+        def quantise_res(n0, n1):
             V.quantize_mx(
-                out=res_codes[:, cols].bitcast(FP8X4),
-                scales=res_scales[PLANE:P, cols],
-                in_=res_bf[h][:, c0:c1, :].rearrange("p n r -> p (n r)"),
+                out=res_codes[:, n0:n1].bitcast(FP8X4),
+                scales=res_scales[PLANE:P, n0:n1],
+                in_=res_bf[:, PACK * n0 : PACK * n1],
             )
 
-        def store_rows(i, r0, r1):
+        def store_rows(i, r0=0, r1=PACK):
             n0, n1 = STORES[i]
             nc.sync.dma_start(out=out_rows[:, r0:r1, n0:n1], in_=res[i][:, r0:r1, :])
 
         def store_words(n0, n1):
             nc.sync.dma_start(out=out_words[:, n0:n1], in_=res_codes[:, n0:n1].bitcast(I32))
 
-        def store_scales(n0, n1, queue):
+        def store_scales(queue):
             for r in range(PACK):
                 queue.dma_start(
-                    out=scale_rows[r][:, n0:n1].bitcast(I32),
-                    in_=res_scales[PLANE + r : P : 32, n0:n1].bitcast(I32),
+                    out=scale_rows[r].bitcast(I32),
+                    in_=res_scales[PLANE + r : P : 32, :].bitcast(I32),
                 )
 
         V.memset(w4s[:].bitcast(I32), 0)
         V.memset(x4s_raw[:].bitcast(I32), 0)
-
         for r in range(2):
             load_scales(w4s, w4_scales, r, nc.gpsimd)
         load_words(x4_raw, x4_words, 0, T)
@@ -266,58 +281,59 @@ def tile_mix_atom_tm_pl_relu2_kernel(
         load_w4(1)
         load_w8(0, 2)
         load_w8(1, 4)
+        load_w8(0, 3)
         load_w8(1, 5)
-
-        def finish(h):
-            rectify(h, 0, S)
-            rectify(h, 1, S)
-            square(h, 0, S)
-            square(h, 1, S)
-
-        deal_x4()
-        group_x8(0, S, 80, P)
-        group_x8(0, V, 0, 80)
-        quantise_x8(0)
-        group_x8(1, S, 80, P)
-        group_x8(1, V, 0, 80)
-        quantise_x8(1)
-        passes4(0, range(PASSES4))
-        passes4(1, range(PASSES4))
-        passes4(2, range(PASSES4))
-        group_w8(0, 0, V, 0, 256)
-        group_w8(1, 0, S, 0, 256)
-        quantise_w8(0, 0)
+        for a in range(PASSES4):
+            deal_x4(a)
+        for g in range(2):
+            group_x8(g, S, 80, P)
+            group_x8(g, V, 0, 80)
+            quantise_x8(g)
+        for h in range(3):
+            passes4(h)
+        group_w8(0, V, 0, 256)
+        group_w8(0, S, 256, 512)
+        quantise_w8(0, 0, 256)
+        pass4(3, 0)
         pass8(0, 0)
-        group_w8(0, 1, V, 0, 256)
-        quantise_w8(1, 0)
-        quantise_w8(0, 1)
+        pass4(3, 1)
+        group_w8(1, V, 0, 256)
+        quantise_w8(0, 256, 512)
+        quantise_w8(1, 0, 256)
         pass8(0, 1)
         pass8(1, 0)
-        group_w8(1, 1, V, 0, 256)
-        quantise_w8(1, 1)
+        group_w8(1, V, 256, 512)
+        quantise_w8(1, 256, 512)
         pass8(1, 1)
-        passes4(3, range(PASSES4))
-        finish(0)
+        pass4(3, 2)
+        rectify(0, 0, S)
+        rectify(0, 1, V)
+        square(0, 0, S)
+        square(0, 1, S)
+        passes4(4)
         finish(1)
-        store_rows(0, 0, PACK)
-
-        group_w8(2, 0, V, 0, 256)
-        group_w8(3, 0, V, 0, 256)
-        group_w8(2, 1, V, 0, 256)
-        quantise_w8(2, 0)
-        quantise_w8(2, 1)
-        passes8(2)
-        group_w8(3, 1, V, 0, 256)
-        quantise_w8(3, 0)
-        quantise_w8(3, 1)
-        passes8(3)
-        passes4(4, range(PASSES4))
-        passes4(5, range(2))
-        group_res(0, V, 0, 256)
-        group_res(1, V, 0, 256)
-        quantise_res(0)
-        quantise_res(1)
-        store_words(0, 512)
+        store_rows(0)
+        group_res(S, 0, 128)
+        group_w8(0, V, 512, 768)
+        group_w8(0, V, 768, 1024)
+        group_w8(1, V, 512, 768)
+        quantise_w8(0, 512, 768)
+        quantise_w8(1, 512, 768)
+        both8(2)
+        group_w8(1, V, 768, 1024)
+        quantise_w8(0, 768, 1024)
+        quantise_w8(1, 768, 1024)
+        both8(3)
+        passes4(5)
+        group_res(V, 128, 256)
+        group_w8(0, V, 1024, 1280)
+        quantise_res(0, 256)
+        quantise_w8(0, 1024, 1280)
+        pass8(4, 0)
+        group_w8(1, V, 1024, 1280)
+        group_res(V, 256, 384)
+        quantise_w8(1, 1024, 1280)
+        pass8(4, 1)
         finish(2)
         rectify(3, 0, S)
         rectify(3, 1, S)
@@ -325,35 +341,31 @@ def tile_mix_atom_tm_pl_relu2_kernel(
         store_rows(1, 0, 2)
         square(3, 1, S)
         store_rows(1, 2, 4)
-        group_res(2, S, 0, 256)
-
-        group_w8(4, 0, V, 0, 256)
-        group_w8(5, 0, V, 0, 256)
-        group_w8(4, 1, V, 0, 256)
-        quantise_w8(4, 0)
-        quantise_w8(4, 1)
-        passes8(4)
-        passes4(5, range(2, PASSES4))
-        group_w8(5, 1, V, 0, 256)
-        quantise_w8(5, 0)
-        quantise_w8(5, 1)
-        passes8(5)
-        group_res(3, V, 0, 256)
-        quantise_res(2)
-        quantise_res(3)
-        store_words(512, 1024)
+        group_w8(0, V, 1280, 1536)
+        group_res(V, 384, 512)
+        quantise_w8(0, 1280, 1536)
+        pass8(5, 0)
+        group_w8(1, V, 1280, 1536)
+        quantise_res(256, 512)
+        quantise_w8(1, 1280, 1536)
+        pass8(5, 1)
+        store_words(0, 512)
+        group_res(V, 512, 768)
+        group_res(V, 768, 1024)
         finish(4)
-        store_rows(2, 0, PACK)
-        rectify(5, 0, V)
-        rectify(5, 1, S)
-        group_res(4, V, 0, 128)
-        square(5, 0, V)
+        store_rows(2)
+        rectify(5, 0, S)
+        rectify(5, 1, V)
+        quantise_res(512, 768)
+        quantise_res(768, 1024)
+        store_words(512, 1024)
+        square(5, 0, S)
         square(5, 1, S)
-        store_rows(3, 0, PACK)
-        group_res(4, V, 128, 256)
-        group_res(5, S, 176, 256)
-        group_res(5, V, 0, 176)
-        quantise_res(4)
-        quantise_res(5)
-        store_scales(0, N, nc.scalar)
+        store_rows(3)
+        group_res(V, 1024, 1280)
+        group_res(S, 1280 + 176, 1536)
+        group_res(V, 1280, 1280 + 176)
+        quantise_res(1024, 1280)
+        quantise_res(1280, 1536)
+        store_scales(nc.scalar)
         store_words(1024, N)

@@ -32,8 +32,9 @@ def spans(*edges):
 
 PIECES = spans(0, 256, 512, 768, 1024, 1280, 1536)
 STORES = spans(0, 512, 1024, 1280, 1536)
-W4_LOADS = spans(0, 1280, 1536)
+W4_LOADS = [(0, 1, 0, 1280), (1, 3, 0, 1280), (0, 3, 1280, 1536)]
 W8_LOADS = [spans(0, 512, 1024, 1280, 1536), PIECES]
+X4_LOADS = spans(0, 1, 3)
 
 
 def holder(table, n):
@@ -53,11 +54,14 @@ def tile_mix_atom_tm_pl_relu2_kernel(
         def tile(name, shape, dtype):
             return sb.tile(shape, dtype, name=name, align_bytes=256)
 
-        x4_raw = tile("x4_raw", [P, PASSES4, 2 * T], U8)
+        x4_raw = [tile("x4_raw%d" % i, [P, a1 - a0, 2 * T], U8) for i, (a0, a1) in enumerate(X4_LOADS)]
         x4_codes = tile("x4_codes", [P, PASSES4, PACK, 2 * P], U8)
         x4s_raw = tile("x4s_raw", [P, PASSES4, T], U8)
         x4s = tile("x4s", [P, PASSES4, PACK, P], U8)
-        w4_parts = [tile("w4_part%d" % i, [P, PASSES4, 2 * (n1 - n0)], U8) for i, (n0, n1) in enumerate(W4_LOADS)]
+        x4s_rows = tile("x4s_rows", [PACK, PASSES4, PACK, T], U8)
+        w4_parts = [
+            tile("w4_part%d" % i, [P, a1 - a0, 2 * (n1 - n0)], U8) for i, (a0, a1, n0, n1) in enumerate(W4_LOADS)
+        ]
         w4s = tile("w4s", [P, PASSES4, N], U8)
         x8_raw = [tile("x8_raw%d" % g, [P, PACK, T], F32) for g in range(PASSES8)]
         x8_bf = [tile("x8_bf%d" % g, [P, T * PACK], BF16) for g in range(PASSES8)]
@@ -101,7 +105,24 @@ def tile_mix_atom_tm_pl_relu2_kernel(
             nc.sync.dma_start(out=dst[:].bitcast(I32), in_=words.bitcast(I32))
 
         def load_w4(i):
-            load_words(w4_parts[i], w4_words, *W4_LOADS[i])
+            a0, a1, n0, n1 = W4_LOADS[i]
+            load_words(w4_parts[i], w4_words[a0:a1], n0, n1)
+
+        def load_x4(i):
+            a0, a1 = X4_LOADS[i]
+            load_words(x4_raw[i], x4_words[a0:a1], 0, T)
+
+        def load_x4_scale_rows(queue):
+            rows = x4_scales.rearrange("a (q r) n -> r (a q) n", r=PACK)
+            queue.dma_start(
+                out=x4s_rows[:].rearrange("r a q n -> r (a q) n").bitcast(I32), in_=rows.bitcast(I32)
+            )
+
+        def spread_x4_scales(a):
+            for q in range(PACK):
+                V.tensor_copy(
+                    out=x4s_raw[32 * q : 32 * q + PACK, a, :].bitcast(I32), in_=x4s_rows[:, a, q, :].bitcast(I32)
+                )
 
         def interleave(engine, dst, src):
             if engine is V:
@@ -117,10 +138,11 @@ def tile_mix_atom_tm_pl_relu2_kernel(
             V.tensor_copy(out=x4s[:, a, :, :], in_=x4s_raw[:, a, :].rearrange("p (m r) -> p r m", r=PACK))
 
         def deal_words(a, engine):
+            i = holder(X4_LOADS, a)
             interleave(
                 engine,
                 x4_codes[:, a, :, :].bitcast(U16),
-                x4_raw[:, a, :].bitcast(U16).rearrange("p (m r) -> p r m", r=PACK),
+                x4_raw[i][:, a - X4_LOADS[i][0], :].bitcast(U16).rearrange("p (m r) -> p r m", r=PACK),
             )
 
         def group_x8(g, engine, m0, m1):
@@ -165,15 +187,15 @@ def tile_mix_atom_tm_pl_relu2_kernel(
 
         def pass4(h, a, token_rows=range(PACK)):
             n0, n1 = PIECES[h]
-            i = holder(W4_LOADS, n0)
-            at = W4_LOADS[i][0]
+            i = max(i for i, (a0, a1, m0, m1) in enumerate(W4_LOADS) if a0 <= a < a1 and m0 <= n0 < m1)
+            a0, at = W4_LOADS[i][0], W4_LOADS[i][2]
             for r in token_rows:
                 multiply(
                     h,
                     r,
                     x4_codes[:, a, r, :].bitcast(FP4X4),
                     x4s[:, a, r, :],
-                    w4_parts[i][:, a, 2 * (n0 - at) : 2 * (n1 - at)].bitcast(FP4X4),
+                    w4_parts[i][:, a - a0, 2 * (n0 - at) : 2 * (n1 - at)].bitcast(FP4X4),
                     w4s[:, a, n0:n1],
                     0,
                     n1 - n0,
@@ -262,14 +284,14 @@ def tile_mix_atom_tm_pl_relu2_kernel(
 
         V.memset(w4s[:].bitcast(I32), 0)
         V.memset(x4s_raw[:].bitcast(I32), 0)
-        for r in range(2):
-            load_scales(w4s, w4_scales, r, nc.gpsimd)
-        load_words(x4_raw, x4_words, 0, T)
+        load_x4(0)
+        load_x4_scale_rows(nc.scalar)
         load_w4(0)
-        for r in range(PACK):
-            load_scales(x4s_raw, x4_scales, r, nc.sync)
-        for r in range(2, PACK):
-            load_scales(w4s, w4_scales, r, nc.sync)
+        for r in range(2):
+            load_scales(w4s, w4_scales, r, nc.scalar)
+            load_scales(w4s, w4_scales, r + 2, nc.sync)
+        load_x4(1)
+        load_w4(1)
         load_x8(0)
         load_x8(1)
         load_w8(0, 0)
@@ -278,25 +300,33 @@ def tile_mix_atom_tm_pl_relu2_kernel(
         load_w8(0, 1)
         load_w8(1, 2)
         load_w8(1, 3)
-        load_w4(1)
+        load_w4(2)
         load_w8(0, 2)
         load_w8(1, 4)
         load_w8(0, 3)
         load_w8(1, 5)
+        spread_x4_scales(0)
+        spread_x4_scales(1)
         for a in range(PASSES4):
-            deal_x4(a)
+            deal_words(a, S)
+            deal_scales(a)
+            if a == 0:
+                spread_x4_scales(2)
         for g in range(2):
             group_x8(g, S, 80, P)
             group_x8(g, V, 0, 80)
             quantise_x8(g)
+        for a in range(2):
+            for h in range(4):
+                pass4(h, a)
         for h in range(3):
-            passes4(h)
+            pass4(h, 2)
         group_w8(0, V, 0, 256)
         group_w8(0, S, 256, 512)
         quantise_w8(0, 0, 256)
-        pass4(3, 0)
         pass8(0, 0)
-        pass4(3, 1)
+        for h in range(3, 4):
+            pass4(h, 2)
         group_w8(1, V, 0, 256)
         quantise_w8(0, 256, 512)
         quantise_w8(1, 0, 256)
@@ -305,7 +335,6 @@ def tile_mix_atom_tm_pl_relu2_kernel(
         group_w8(1, V, 256, 512)
         quantise_w8(1, 256, 512)
         pass8(1, 1)
-        pass4(3, 2)
         rectify(0, 0, S)
         rectify(0, 1, V)
         square(0, 0, S)
@@ -352,19 +381,19 @@ def tile_mix_atom_tm_pl_relu2_kernel(
         store_words(0, 512)
         group_res(V, 512, 768)
         group_res(V, 768, 1024)
+        quantise_res(512, 768)
         finish(4)
         store_rows(2)
-        rectify(5, 0, S)
-        rectify(5, 1, V)
-        quantise_res(512, 768)
+        rectify(5, 0, V)
         quantise_res(768, 1024)
         store_words(512, 1024)
-        square(5, 0, S)
+        rectify(5, 1, S)
+        square(5, 0, V)
         square(5, 1, S)
         store_rows(3)
         group_res(V, 1024, 1280)
-        group_res(S, 1280 + 176, 1536)
-        group_res(V, 1280, 1280 + 176)
+        group_res(S, 1280 + 128, 1536)
+        group_res(V, 1280, 1280 + 128)
         quantise_res(1024, 1280)
         quantise_res(1280, 1536)
         store_scales(nc.scalar)

@@ -32,9 +32,9 @@ def spans(*edges):
 
 PIECES = spans(0, 256, 512, 768, 1024, 1280, 1536)
 STORES = spans(0, 512, 1024, 1280, 1536)
+X4_LOADS = spans(0, 3)
 W4_LOADS = [(0, 1, 0, 1280), (1, 3, 0, 1280), (0, 3, 1280, 1536)]
-W8_LOADS = [spans(0, 512, 1024, 1280, 1536), PIECES]
-X4_LOADS = spans(0, 1, 3)
+W8_LOADS = [spans(0, 512, 1024, 1536), spans(0, 256, 512, 768, 1024, 1280, 1536)]
 
 
 def holder(table, n):
@@ -284,13 +284,13 @@ def tile_mix_atom_tm_pl_relu2_kernel(
 
         V.memset(w4s[:].bitcast(I32), 0)
         V.memset(x4s_raw[:].bitcast(I32), 0)
+        load_scales(w4s, w4_scales, 0, nc.gpsimd)
         load_x4(0)
         load_x4_scale_rows(nc.scalar)
         load_w4(0)
-        for r in range(2):
-            load_scales(w4s, w4_scales, r, nc.scalar)
-            load_scales(w4s, w4_scales, r + 2, nc.sync)
-        load_x4(1)
+        load_scales(w4s, w4_scales, 1, nc.scalar)
+        load_scales(w4s, w4_scales, 2, nc.sync)
+        load_scales(w4s, w4_scales, 3, nc.sync)
         load_w4(1)
         load_x8(0)
         load_x8(1)
@@ -303,15 +303,11 @@ def tile_mix_atom_tm_pl_relu2_kernel(
         load_w4(2)
         load_w8(0, 2)
         load_w8(1, 4)
-        load_w8(0, 3)
         load_w8(1, 5)
-        spread_x4_scales(0)
-        spread_x4_scales(1)
         for a in range(PASSES4):
-            deal_words(a, S)
-            deal_scales(a)
-            if a == 0:
-                spread_x4_scales(2)
+            spread_x4_scales(a)
+        for a in range(PASSES4):
+            deal_x4(a)
         for g in range(2):
             group_x8(g, S, 80, P)
             group_x8(g, V, 0, 80)
@@ -319,81 +315,80 @@ def tile_mix_atom_tm_pl_relu2_kernel(
         for a in range(2):
             for h in range(4):
                 pass4(h, a)
-        for h in range(3):
-            pass4(h, 2)
+        pass4(0, 2)
+        pass4(1, 2)
+        pass4(2, 2)
         group_w8(0, V, 0, 256)
         group_w8(0, S, 256, 512)
         quantise_w8(0, 0, 256)
         pass8(0, 0)
-        for h in range(3, 4):
-            pass4(h, 2)
-        group_w8(1, V, 0, 256)
+        group_w8(1, V, 0, 176)
+        group_w8(1, S, 176, 256)
         quantise_w8(0, 256, 512)
         quantise_w8(1, 0, 256)
         pass8(0, 1)
+        pass4(3, 2)
         pass8(1, 0)
-        group_w8(1, V, 256, 512)
+        group_w8(1, S, 256+128, 512)
+        group_w8(1, V, 256, 256+128)
         quantise_w8(1, 256, 512)
         pass8(1, 1)
-        rectify(0, 0, S)
-        rectify(0, 1, V)
-        square(0, 0, S)
-        square(0, 1, S)
-        passes4(4)
+        finish(0)
         finish(1)
+        pass4(4, 0)
+        pass4(4, 1)
         store_rows(0)
-        group_res(S, 0, 128)
+        group_res(S, 0, 256)
         group_w8(0, V, 512, 768)
         group_w8(0, V, 768, 1024)
         group_w8(1, V, 512, 768)
         quantise_w8(0, 512, 768)
         quantise_w8(1, 512, 768)
         both8(2)
+        pass4(4, 2)
         group_w8(1, V, 768, 1024)
         quantise_w8(0, 768, 1024)
         quantise_w8(1, 768, 1024)
         both8(3)
-        passes4(5)
-        group_res(V, 128, 256)
-        group_w8(0, V, 1024, 1280)
+        pass4(5, 0)
+        pass4(5, 1)
+        pass4(5, 2)
+        group_res(V, 256, 512)
         quantise_res(0, 256)
-        quantise_w8(0, 1024, 1280)
-        pass8(4, 0)
-        group_w8(1, V, 1024, 1280)
-        group_res(V, 256, 384)
-        quantise_w8(1, 1024, 1280)
-        pass8(4, 1)
+        quantise_res(256, 512)
+        store_words(0, 512)
         finish(2)
-        rectify(3, 0, S)
-        rectify(3, 1, S)
-        square(3, 0, S)
-        store_rows(1, 0, 2)
-        square(3, 1, S)
-        store_rows(1, 2, 4)
+        finish(3)
+        store_rows(1)
+        group_res(S, 512, 768)
+        group_w8(0, V, 1024, 1280)
         group_w8(0, V, 1280, 1536)
-        group_res(V, 384, 512)
+        quantise_w8(0, 1024, 1280)
+        group_w8(1, V, 1024, 1280)
         quantise_w8(0, 1280, 1536)
+        quantise_w8(1, 1024, 1280)
+        pass8(4, 0)
+        pass8(4, 1)
         pass8(5, 0)
         group_w8(1, V, 1280, 1536)
-        quantise_res(256, 512)
+        group_res(V, 768, 896)
         quantise_w8(1, 1280, 1536)
         pass8(5, 1)
-        store_words(0, 512)
-        group_res(V, 512, 768)
-        group_res(V, 768, 1024)
+        group_res(V, 896, 1024)
         quantise_res(512, 768)
+        quantise_res(768, 1024)
+        store_words(512, 1024)
         finish(4)
         store_rows(2)
         rectify(5, 0, V)
-        quantise_res(768, 1024)
-        store_words(512, 1024)
-        rectify(5, 1, S)
-        square(5, 0, V)
-        square(5, 1, S)
+        rectify(5, 1, V)
+        square(5, 0, S)
+        square(5, 1, V)
         store_rows(3)
-        group_res(V, 1024, 1280)
-        group_res(S, 1280 + 128, 1536)
-        group_res(V, 1280, 1280 + 128)
+        group_res(S, 1024, 1120)
+        group_res(V, 1120, 1280)
+        group_res(S, 1280 + 176, 1536)
+        group_res(V, 1280, 1280 + 176)
         quantise_res(1024, 1280)
         quantise_res(1280, 1536)
         store_scales(nc.scalar)

@@ -249,6 +249,14 @@ def tile_mix_atom_tm_pl_relu2_kernel(
             else:
                 S.activation(out=dst, in_=src, func=ACT.Square)
 
+        def square_row(h, r, engine):
+            src = relu[h][:, r, :]
+            dst = result(*PIECES[h])[:, r, :]
+            if engine is V:
+                V.tensor_tensor(out=dst, in0=src, in1=src, op=ALU.mult)
+            else:
+                S.activation(out=dst, in_=src, func=ACT.Square)
+
         def finish(h, engine=S):
             banks = range(PACK * width[h] // BANK)
             for b in banks:
@@ -309,8 +317,8 @@ def tile_mix_atom_tm_pl_relu2_kernel(
         for a in range(PASSES4):
             deal_x4(a)
         for g in range(2):
-            group_x8(g, S, 80, P)
-            group_x8(g, V, 0, 80)
+            group_x8(g, S, 88, P)
+            group_x8(g, V, 0, 88)
             quantise_x8(g)
         for a in range(2):
             for h in range(4):
@@ -322,23 +330,24 @@ def tile_mix_atom_tm_pl_relu2_kernel(
         group_w8(0, S, 256, 512)
         quantise_w8(0, 0, 256)
         pass8(0, 0)
-        group_w8(1, V, 0, 176)
-        group_w8(1, S, 176, 256)
+        group_w8(1, V, 0, 256)
         quantise_w8(0, 256, 512)
         quantise_w8(1, 0, 256)
         pass8(0, 1)
-        pass4(3, 2)
         pass8(1, 0)
-        group_w8(1, S, 256+128, 512)
-        group_w8(1, V, 256, 256+128)
+        group_w8(1, V, 256, 512)
         quantise_w8(1, 256, 512)
         pass8(1, 1)
-        finish(0)
+        rectify(0, 0, S)
+        rectify(0, 1, V)
+        square(0, 0, S)
+        square(0, 1, S)
         finish(1)
+        pass4(3, 2)
         pass4(4, 0)
         pass4(4, 1)
         store_rows(0)
-        group_res(S, 0, 256)
+        group_res(S, 0, 128)
         group_w8(0, V, 512, 768)
         group_w8(0, V, 768, 1024)
         group_w8(1, V, 512, 768)
@@ -353,6 +362,7 @@ def tile_mix_atom_tm_pl_relu2_kernel(
         pass4(5, 0)
         pass4(5, 1)
         pass4(5, 2)
+        group_res(V, 128, 256)
         group_res(V, 256, 512)
         quantise_res(0, 256)
         quantise_res(256, 512)

from contextlib import ExitStack

import concourse.mybir as mybir

O, K4, N, T = 1024, 1536, 1536, 512
FLOPS = 2 * (O + K4) * N * T

F32 = mybir.dt.float32
BF16 = mybir.dt.bfloat16
I32 = mybir.dt.int32
U32 = mybir.dt.uint32
U16 = mybir.dt.uint16
U8 = mybir.dt.uint8
FP8X4 = mybir.dt.float8_e4m3fn_x4
FP4X4 = mybir.dt.float4_e2m1fn_x4
ACT = mybir.ActivationFunctionType
ALU = mybir.AluOpType

P = 128
PACK = 4
K_PASS = P * PACK
PASSES8 = O // K_PASS
PASSES4 = K4 // K_PASS
BANK = 512
BANKS = 8
PLANE = 4


def spans(*edges):
    return list(zip(edges[:-1], edges[1:]))


PIECES = spans(0, 256, 512, 768, 1024, 1280, 1536)
STORES = spans(0, 512, 1024, 1280, 1536)
X4_LOADS = spans(0, 3)
W4_LOADS = [(0, 1, 0, 1280), (1, 3, 0, 1280), (0, 3, 1280, 1536)]
W8_LOADS = [spans(0, 512, 1024, 1536), spans(0, 256, 512, 768, 1024, 1280, 1536)]


def holder(table, n):
    return max(i for i, (n0, n1) in enumerate(table) if n0 <= n)


def tile_mix_atom_tm_pl_relu2_kernel(
    tc, x8, w8, x4_words, x4_scales, w4_words, w4_scales, out_0, out_1, out_2
):
    nc = tc.nc
    with ExitStack() as ctx:
        sb = ctx.enter_context(tc.tile_pool(name="sb", bufs=1))
        psum = ctx.enter_context(tc.psum_pool(name="psum", bufs=1))
        ctx.enter_context(tc.manual_schedule())
        V, S = nc.vector, nc.scalar

        def tile(name, shape, dtype):
            return sb.tile(shape, dtype, name=name, align_bytes=256)

        x4_raw = [tile("x4_raw%d" % i, [P, a1 - a0, 2 * T], U8) for i, (a0, a1) in enumerate(X4_LOADS)]
        x4_codes = tile("x4_codes", [P, PASSES4, PACK, 2 * P], U8)
        x4s_raw = tile("x4s_raw", [P, PASSES4, T], U8)
        x4s = tile("x4s", [P, PASSES4, PACK, P], U8)
        x4s_rows = tile("x4s_rows", [PACK, PASSES4, PACK, T], U8)
        w4_parts = [
            tile("w4_part%d" % i, [P, a1 - a0, 2 * (n1 - n0)], U8) for i, (a0, a1, n0, n1) in enumerate(W4_LOADS)
        ]
        w4s = tile("w4s", [P, PASSES4, N], U8)
        x8_raw = [tile("x8_raw%d" % g, [P, PACK, T], F32) for g in range(PASSES8)]
        x8_bf = [tile("x8_bf%d" % g, [P, T * PACK], BF16) for g in range(PASSES8)]
        x8_codes = [tile("x8_codes%d" % g, [P, T], U32) for g in range(PASSES8)]
        x8s = [tile("x8s%d" % g, [P, T], U8) for g in range(PASSES8)]
        w8_raw = [
            [tile("w8_raw%d_%d" % (g, n0), [P, PACK, n1 - n0], F32) for n0, n1 in W8_LOADS[g]] for g in range(PASSES8)
        ]
        w8_bf = [tile("w8_bf%d" % g, [P, N * PACK], BF16) for g in range(PASSES8)]
        w8_codes = [tile("w8_codes%d" % g, [P, N], U32) for g in range(PASSES8)]
        w8s = [tile("w8s%d" % g, [P, N], U8) for g in range(PASSES8)]
        width = [n1 - n0 for n0, n1 in PIECES]
        relu = [tile("relu%d" % h, [P, PACK, w], F32) for h, w in enumerate(width)]
        res = [tile("res%d" % i, [P, PACK, n1 - n0], F32) for i, (n0, n1) in enumerate(STORES)]
        res_bf = tile("res_bf", [P, N * PACK], BF16)
        res_codes = tile("res_codes", [P, N], U32)
        res_scales = tile("res_scales", [P, N], U8)
        acc = {}
        done = {}

        out_rows = out_0.rearrange("(p r) n -> p r n", r=PACK)
        out_words = out_1[0].rearrange("p n i -> p (n i)").bitcast(I32)
        scale_rows = out_2[0].rearrange("(q r) n -> r q n", r=PACK)

        def load_scales(plane, src, r, queue):
            rows = src.rearrange("a (q r) n -> r q a n", r=PACK)[r]
            queue.dma_start(out=plane[r:P:32, :, :].bitcast(I32), in_=rows.bitcast(I32))

        def load_rows(raw, src, g, n0, n1):
            rows = src[g * K_PASS : (g + 1) * K_PASS, n0:n1]
            nc.sync.dma_start(out=raw[:], in_=rows.rearrange("(p j) n -> p j n", j=PACK))

        def load_x8(g):
            load_rows(x8_raw[g], x8, g, 0, T)

        def load_w8(g, i):
            load_rows(w8_raw[g][i], w8, g, *W8_LOADS[g][i])

        def load_words(dst, src, n0, n1):
            words = src[:, :, 2 * n0 : 2 * n1].rearrange("a p w -> p a w")
            nc.sync.dma_start(out=dst[:].bitcast(I32), in_=words.bitcast(I32))

        def load_w4(i):
            a0, a1, n0, n1 = W4_LOADS[i]
            load_words(w4_parts[i], w4_words[a0:a1], n0, n1)

        def load_x4(i):
            a0, a1 = X4_LOADS[i]
            load_words(x4_raw[i], x4_words[a0:a1], 0, T)

        def load_x4_scale_rows(queue):
            rows = x4_scales.rearrange("a (q r) n -> r (a q) n", r=PACK)
            queue.dma_start(
                out=x4s_rows[:].rearrange("r a q n -> r (a q) n").bitcast(I32), in_=rows.bitcast(I32)
            )

        def spread_x4_scales(a):
            for q in range(PACK):
                V.tensor_copy(
                    out=x4s_raw[32 * q : 32 * q + PACK, a, :].bitcast(I32), in_=x4s_rows[:, a, q, :].bitcast(I32)
                )

        def interleave(engine, dst, src):
            if engine is V:
                V.tensor_copy(out=dst, in_=src)
            else:
                S.copy(out=dst, in_=src)

        def deal_x4(a):
            V.tensor_copy(out=x4s[:, a, :, :], in_=x4s_raw[:, a, :].rearrange("p (m r) -> p r m", r=PACK))
            deal_words(a, V)

        def deal_scales(a):
            V.tensor_copy(out=x4s[:, a, :, :], in_=x4s_raw[:, a, :].rearrange("p (m r) -> p r m", r=PACK))

        def deal_words(a, engine):
            i = holder(X4_LOADS, a)
            interleave(
                engine,
                x4_codes[:, a, :, :].bitcast(U16),
                x4_raw[i][:, a - X4_LOADS[i][0], :].bitcast(U16).rearrange("p (m r) -> p r m", r=PACK),
            )

        def group_x8(g, engine, m0, m1):
            dst = x8_bf[g][:].rearrange("p (r m j) -> p m j r", r=PACK, j=PACK)[:, m0:m1, :, :]
            src = x8_raw[g][:].rearrange("p j (m r) -> p m j r", r=PACK)[:, m0:m1, :, :]
            interleave(engine, dst, src)

        def quantise_x8(g):
            V.quantize_mx(out=x8_codes[g][:].bitcast(FP8X4), scales=x8s[g][:], in_=x8_bf[g][:])

        def group_w8(g, engine, n0, n1):
            i = holder(W8_LOADS[g], n0)
            at = W8_LOADS[g][i][0]
            dst = w8_bf[g][:, PACK * n0 : PACK * n1].rearrange("p (m i j) -> p m j i", i=PACK, j=PACK)
            src = w8_raw[g][i][:, :, n0 - at : n1 - at].rearrange("p j (m i) -> p m j i", i=PACK)
            interleave(engine, dst, src)

        def quantise_w8(g, n0, n1):
            V.quantize_mx(
                out=w8_codes[g][:, n0:n1].bitcast(FP8X4),
                scales=w8s[g][:, n0:n1],
                in_=w8_bf[g][:, PACK * n0 : PACK * n1],
            )

        def multiply(h, r, lhsT, lhsT_scale, rhs, rhs_scale, c0, c1):
            rows = BANK // width[h]
            b = r // rows
            first = (h, b) not in acc
            if first:
                acc[h, b] = psum.tile([P, rows, width[h]], F32, name="acc%d" % (len(acc) % BANKS))
                done[h, b] = 0
            done[h, b] = done[h, b] + c1 - c0
            nc.tensor.matmul_mx(
                out=acc[h, b][:, r % rows, c0:c1],
                lhsT=lhsT,
                lhsT_scale=lhsT_scale,
                rhs=rhs,
                rhs_scale=rhs_scale,
                start=first,
                stop=done[h, b] == (PASSES4 + PASSES8) * BANK,
            )

        def pass4(h, a, token_rows=range(PACK)):
            n0, n1 = PIECES[h]
            i = max(i for i, (a0, a1, m0, m1) in enumerate(W4_LOADS) if a0 <= a < a1 and m0 <= n0 < m1)
            a0, at = W4_LOADS[i][0], W4_LOADS[i][2]
            for r in token_rows:
                multiply(
                    h,
                    r,
                    x4_codes[:, a, r, :].bitcast(FP4X4),
                    x4s[:, a, r, :],
                    w4_parts[i][:, a - a0, 2 * (n0 - at) : 2 * (n1 - at)].bitcast(FP4X4),
                    w4s[:, a, n0:n1],
                    0,
                    n1 - n0,
                )

        def passes4(h):
            for a in range(PASSES4):
                pass4(h, a)

        def pass8(h, g, token_rows=range(PACK), c0=0, c1=None):
            n0, n1 = PIECES[h]
            c1 = n1 - n0 if c1 is None else c1
            for r in token_rows:
                multiply(
                    h,
                    r,
                    x8_codes[g][:, r * P : (r + 1) * P].bitcast(FP8X4),
                    x8s[g][:, r * P : (r + 1) * P],
                    w8_codes[g][:, n0 + c0 : n0 + c1].bitcast(FP8X4),
                    w8s[g][:, n0 + c0 : n0 + c1],
                    c0,
                    c1,
                )

        def both8(h):
            rows = BANK // width[h]
            for r in range(0, PACK, rows):
                for g in range(PASSES8):
                    pass8(h, g, range(r, r + rows))

        def result(n0, n1):
            i = holder(STORES, n0)
            return res[i][:, :, n0 - STORES[i][0] : n1 - STORES[i][0]]

        def bank_rows(h, b):
            rows = BANK // width[h]
            return slice(b * rows, (b + 1) * rows)

        def rectify(h, b, engine):
            dst = relu[h][:, bank_rows(h, b), :]
            if engine is V:
                V.tensor_scalar(out=dst, in0=acc[h, b][:], scalar1=0.0, scalar2=None, op0=ALU.max)
            else:
                S.activation(out=dst, in_=acc[h, b][:], func=ACT.Relu)

        def square(h, b, engine):
            src = relu[h][:, bank_rows(h, b), :]
            dst = result(*PIECES[h])[:, bank_rows(h, b), :]
            if engine is V:
                V.tensor_tensor(out=dst, in0=src, in1=src, op=ALU.mult)
            else:
                S.activation(out=dst, in_=src, func=ACT.Square)

        def square_row(h, r, engine):
            src = relu[h][:, r, :]
            dst = result(*PIECES[h])[:, r, :]
            if engine is V:
                V.tensor_tensor(out=dst, in0=src, in1=src, op=ALU.mult)
            else:
                S.activation(out=dst, in_=src, func=ACT.Square)

        def finish(h, engine=S):
            banks = range(PACK * width[h] // BANK)
            for b in banks:
                rectify(h, b, engine)
            for b in banks:
                square(h, b, engine)

        def group_res(engine, n0, n1):
            dst = res_bf[:, PACK * n0 : PACK * n1].rearrange("p (m i r) -> p m r i", i=PACK, r=PACK)
            src = result(n0, n1).rearrange("p r (m i) -> p m r i", i=PACK)
            interleave(engine, dst, src)

        def quantise_res(n0, n1):
            V.quantize_mx(
                out=res_codes[:, n0:n1].bitcast(FP8X4),
                scales=res_scales[PLANE:P, n0:n1],
                in_=res_bf[:, PACK * n0 : PACK * n1],
            )

        def store_rows(i, r0=0, r1=PACK):
            n0, n1 = STORES[i]
            nc.sync.dma_start(out=out_rows[:, r0:r1, n0:n1], in_=res[i][:, r0:r1, :])

        def store_words(n0, n1):
            nc.sync.dma_start(out=out_words[:, n0:n1], in_=res_codes[:, n0:n1].bitcast(I32))

        def store_scales(queue):
            for r in range(PACK):
                queue.dma_start(
                    out=scale_rows[r].bitcast(I32),
                    in_=res_scales[PLANE + r : P : 32, :].bitcast(I32),
                )

        V.memset(w4s[:].bitcast(I32), 0)
        V.memset(x4s_raw[:].bitcast(I32), 0)
        load_scales(w4s, w4_scales, 0, nc.gpsimd)
        load_x4(0)
        load_x4_scale_rows(nc.scalar)
        load_w4(0)
        load_scales(w4s, w4_scales, 1, nc.scalar)
        load_scales(w4s, w4_scales, 2, nc.sync)
        load_scales(w4s, w4_scales, 3, nc.sync)
        load_w4(1)
        load_x8(0)
        load_x8(1)
        load_w8(0, 0)
        load_w8(1, 0)
        load_w8(1, 1)
        load_w8(0, 1)
        load_w8(1, 2)
        load_w8(1, 3)
        load_w4(2)
        load_w8(0, 2)
        load_w8(1, 4)
        load_w8(1, 5)
        for a in range(PASSES4):
            spread_x4_scales(a)
        for a in range(PASSES4):
            deal_x4(a)
        for g in range(2):
            group_x8(g, S, 88, P)
            group_x8(g, V, 0, 88)
            quantise_x8(g)
        for a in range(2):
            for h in range(4):
                pass4(h, a)
        pass4(0, 2)
        pass4(1, 2)
        pass4(2, 2)
        group_w8(0, V, 0, 256)
        group_w8(0, S, 256, 512)
        quantise_w8(0, 0, 256)
        pass8(0, 0)
        group_w8(1, V, 0, 256)
        quantise_w8(0, 256, 512)
        quantise_w8(1, 0, 256)
        pass8(0, 1)
        pass8(1, 0)
        group_w8(1, V, 256, 512)
        quantise_w8(1, 256, 512)
        pass8(1, 1)
        rectify(0, 0, S)
        rectify(0, 1, V)
        square(0, 0, S)
        square(0, 1, S)
        finish(1)
        pass4(3, 2)
        pass4(4, 0)
        pass4(4, 1)
        store_rows(0)
        group_res(S, 0, 128)
        group_w8(0, V, 512, 768)
        group_w8(0, V, 768, 1024)
        group_w8(1, V, 512, 768)
        quantise_w8(0, 512, 768)
        quantise_w8(1, 512, 768)
        both8(2)
        pass4(4, 2)
        group_w8(1, V, 768, 1024)
        quantise_w8(0, 768, 1024)
        quantise_w8(1, 768, 1024)
        both8(3)
        pass4(5, 0)
        pass4(5, 1)
        pass4(5, 2)
        group_res(V, 128, 256)
        group_res(V, 256, 512)
        quantise_res(0, 256)
        quantise_res(256, 512)
        store_words(0, 512)
        finish(2)
        finish(3)
        store_rows(1)
        group_res(S, 512, 768)
        group_w8(0, V, 1024, 1280)
        group_w8(0, V, 1280, 1536)
        quantise_w8(0, 1024, 1280)
        group_w8(1, V, 1024, 1280)
        quantise_w8(0, 1280, 1536)
        quantise_w8(1, 1024, 1280)
        pass8(4, 0)
        pass8(4, 1)
        pass8(5, 0)
        group_w8(1, V, 1280, 1536)
        group_res(V, 768, 896)
        quantise_w8(1, 1280, 1536)
        pass8(5, 1)
        group_res(V, 896, 1024)
        quantise_res(512, 768)
        quantise_res(768, 1024)
        store_words(512, 1024)
        finish(4)
        store_rows(2)
        rectify(5, 0, V)
        rectify(5, 1, V)
        square(5, 0, S)
        square(5, 1, V)
        store_rows(3)
        group_res(S, 1024, 1120)
        group_res(V, 1120, 1280)
        group_res(S, 1280 + 176, 1536)
        group_res(V, 1280, 1280 + 176)
        quantise_res(1024, 1280)
        quantise_res(1280, 1536)
        store_scales(nc.scalar)
        store_words(1024, N)
